import numpy as np
CORES = [22,46,70,150,174,198,278,302,326,406,430,454]
N = 12
T = 1024
def entries(a): return a.T.reshape(-1)
def pack(v, P): return np.ascontiguousarray(np.asarray(v, np.int32).reshape(-1, P).T)
def lists(rng, how):
    h = rng.integers(0, N * T, 8)
    if how == "zero": h[:] = 0
    if how == "blocks": h = T * rng.integers(1, N, 8)
    if how == "last": h[:] = N * T - 1
    if how == "mixed": h = T * rng.choice([q for q in range(N) if q & (q - 1)], 8) + rng.integers(1, T, 8)
    if how == "small": h = rng.integers(1, T, 8)
    h[1:] = 0
    return {"hh": np.broadcast_to(pack(np.concatenate([h, np.zeros(24, np.int64)]), 16), (N, 16, 2)).copy()}
def setup_inputs(rng):
    return dict({"x": rng.standard_normal((N, 128, T), dtype=np.float32)}, **lists(rng, "uniform"))
def setup_inputs_blocks(rng):
    d = setup_inputs(rng); d.update(lists(rng, "blocks"))
    for k in ("x",): d[k] = (d[k].astype(np.float32) * 1048576.0).astype(d[k].dtype)
    return d
def setup_inputs_last(rng):
    d = setup_inputs(rng); d.update(lists(rng, "last"))
    for k in ("x",): d[k] = (d[k].astype(np.float32) * (1 / 1024.0)).astype(d[k].dtype)
    return d
def setup_inputs_mixed(rng):
    d = setup_inputs(rng); d.update(lists(rng, "mixed"))
    return d
def setup_inputs_small(rng):
    d = setup_inputs(rng); d.update(lists(rng, "small"))
    return d
def setup_inputs_zero(rng):
    d = setup_inputs(rng); d.update(lists(rng, "zero"))
    return d
def check_inputs(x):
    bad = []
    if x["hh"].min() < 0 or x["hh"].max() >= N * T: bad.append("hh out of range")
    if entries(x["hh"][0])[1:].any(): bad.append("an entry that should be 0 isn't")
    if not all(np.array_equal(a, x["hh"][0]) for a in x["hh"]): bad.append("hh isn't alike on all ranks")
    return bad
def reference(x, hh):
    h = entries(hh[0]); A = np.concatenate(list(x), axis=1)
    Y = np.roll(A, -int(h[0]), axis=1)
    return {"y": np.stack([Y[:, T * r:T * r + T] for r in range(N)])}

@@ -1,0 +1,198 @@
+from concourse.bass import DstId, RemoteDMATransfer
+from concourse.mybir import AluOpType, ActivationFunctionType
+
+NR = 12
+TC = 1024
+SET = 6
+SLICES = [(0, 352), (352, 688), (688, 1024)]
+STR = 22
+SHIFT = 3
+
+SCRATCH = {
+    "xs": ("sbuf", [128, TC], "float32"),
+    "bl": ("sbuf", [128, SET * 352], "float32"),
+    "gt": ("sbuf", [128, SET * 352], "float32"),
+    "rv": ("sbuf", [128, 2 * TC], "float32"),
+    "yb": ("sbuf", [128, TC], "float32"),
+    "ht": ("sbuf", [16, 2], "int32"),
+    "hb": ("sbuf", [128, 2], "int32"),
+    "pi": ("sbuf", [128, 1], "int32"),
+    "pf": ("sbuf", [128, 1], "float32"),
+    "sq": ("sbuf", [128, 2], "int32"),
+    "sf": ("sbuf", [128, 2], "float32"),
+    "hf": ("sbuf", [128, 1], "float32"),
+    "qt": ("sbuf", [128, 1], "float32"),
+    "r6": ("sbuf", [128, SET * STR], "float32"),
+    "ec": ("sbuf", [128, SET * STR], "float32"),
+    "u1": ("sbuf", [128, SET * STR], "float32"),
+    "u2": ("sbuf", [128, SET * STR], "float32"),
+    "jj": ("sbuf", [128, 64], "float32"),
+    "ji": ("sbuf", [128, 64], "int32"),
+    "jr": ("sbuf", [128, 64], "int32"),
+    "a1": ("sbuf", [128, 64], "float32"),
+    "a2": ("sbuf", [128, 64], "float32"),
+    "a3": ("sbuf", [128, 64], "float32"),
+    "offi": ("sbuf", [128, SET * STR], "uint16"),
+    "offf": ("sbuf", [128, 64], "uint16"),
+}
+SEMAPHORES = ["lh", "lx0", "lx1", "lx2", "tab", "hb", "v", "li", "lf", "arr1", "arr2", "ls", "own", "f0", "f1", "f2",
+              "st", "g0", "g1", "g2", "g3", "g4"]
+
+
+def half_of(q):
+    return ((q + SHIFT) % NR) // SET
+
+
+def rank_program(g, core, T, topo):
+    rank = T.rank_of(core)
+    if rank is None:
+        return
+    S = T.sem
+    V, A = g.vector, g.scalar
+    cores = T.cores
+    copy = ActivationFunctionType.Copy
+    ranks = list(range(NR))
+    own = [r for r in ranks if topo.host(cores[r]) == topo.host(core)]
+    rack = [r for r in ranks if topo.rack(topo.host(cores[r])) == topo.rack(topo.host(core))]
+    cabled = [r for r in ranks if r not in rack and topo.may_write(core, cores[r])]
+    m = own.index(rank)
+    lo, hi = SLICES[m]
+    W = hi - lo
+    place = (rank + SHIFT) % SET
+    myhalf = half_of(rank)
+
+    order = [(m + 1) % 3, (m + 2) % 3, m]
+    srcs = []
+    for mm in order:
+        a, b = SLICES[mm]
+        srcs.append(T.bl[:, place * W:(place + 1) * W] if mm == m else T.xs[:, a:b])
+    a, b = SLICES[order[0]]
+    g.sync.dma_start(out=srcs[0], in_=T.x[:, a:b]).then_inc(S.lx0, 16)
+    a, b = SLICES[order[1]]
+    A.dma_start(out=srcs[1], in_=T.x[:, a:b]).then_inc(S.lx1, 16)
+    a, b = SLICES[order[2]]
+    g.sync.dma_start(out=srcs[2], in_=T.x[:, a:b]).then_inc(S.lx2, 16)
+    A.dma_start(out=T.ht[:], in_=T.hh[:]).then_inc(S.lh, 16)
+
+    base = (TC * rank + SHIFT * TC) % (NR * TC)
+    g.iota(T.pi[:], [[0, 1]], 0, 1).then_inc(S.tab, 1)
+    g.iota(T.r6[:], [[0, SET], [16, STR]], lo, 0, allow_small_or_imprecise_dtypes=True).then_inc(S.tab, 1)
+    g.iota(T.ec[:], [[W, SET], [16, STR]], 0, 0, allow_small_or_imprecise_dtypes=True).then_inc(S.tab, 1)
+    g.iota(T.jj[:], [[16, 64]], base, 0, allow_small_or_imprecise_dtypes=True).then_inc(S.tab, 1)
+
+    for k, mm in enumerate(order):
+        ma, mb = SLICES[mm]
+        mw = mb - ma
+        peers = [grp[mm] for grp in (cabled, own) if grp[mm] != rank]
+        ids, dsts, mask = [], [], None
+        for r in peers:
+            rid, pid = topo.addr(cores[r], core)
+            ids.append(DstId(rid=rid, pnc=pid))
+            dsts.append(T.bl[:, place * mw:(place + 1) * mw])
+            mk = topo.mask(core, cores[r])
+            mask = mk if mask is None else mask & mk
+        g.wait_ge(S["lx%d" % k], 16)
+        g.remote_dma_fused([RemoteDMATransfer(dst_ids=ids, dma_engine_mask=mask, remote_sem=S.arr1,
+                                              srcs=[srcs[k]], dsts=dsts)], local_sem=S.ls)
+
+    g.wait_ge(S.lh, 16)
+    g.partition_broadcast(T.hb[:], T.ht[0:1, :], 128).then_inc(S.hb, 1)
+
+    nv = [0]
+
+    def step(ins):
+        nv[0] += 1
+        ins.then_inc(S.v, 1)
+
+    def sync_v():
+        V.wait_ge(S.v, nv[0])
+
+    V.wait_ge(S.tab, 4)
+    step(V.tensor_scalar(T.pi[:], T.pi[:], 15, None, AluOpType.bitwise_and))
+    sync_v()
+    step(V.tensor_copy(T.pf[:], T.pi[:]))
+    sync_v()
+    for t in (T.r6, T.ec, T.jj):
+        step(V.tensor_scalar(t[:], t[:], T.pf[:], None, AluOpType.add))
+    V.wait_ge(S.hb, 1)
+    step(V.tensor_scalar(T.sq[:, 0:1], T.hb[:, 0:1], TC - 1, None, AluOpType.bitwise_and))
+    step(V.tensor_scalar(T.sq[:, 1:2], T.hb[:, 0:1], 10, None, AluOpType.logical_shift_right))
+    step(V.tensor_copy(T.hf[:], T.hb[:, 0:1]))
+    sync_v()
+    step(V.tensor_copy(T.sf[:], T.sq[:]))
+    sync_v()
+    step(V.tensor_scalar(T.qt[:], T.sf[:, 1:2], float(SET), float(-SET), AluOpType.is_ge, AluOpType.mult))
+    sync_v()
+    step(V.tensor_tensor(T.qt[:], T.qt[:], T.sf[:, 1:2], AluOpType.add))
+    sync_v()
+    step(V.tensor_scalar(T.u1[:], T.r6[:], T.sf[:, 0:1], T.qt[:], AluOpType.is_lt, AluOpType.add))
+    sync_v()
+    step(V.tensor_scalar(T.u1[:], T.u1[:], float(W), None, AluOpType.mult))
+    sync_v()
+    step(V.tensor_tensor(T.u1[:], T.u1[:], T.ec[:], AluOpType.add))
+    sync_v()
+    step(V.tensor_scalar(T.u2[:], T.u1[:], float(SET * W), float(-SET * W), AluOpType.is_ge, AluOpType.mult))
+    sync_v()
+    step(V.tensor_tensor(T.u1[:], T.u1[:], T.u2[:], AluOpType.add))
+    sync_v()
+    V.tensor_copy(T.offi[:], T.u1[:]).then_inc(S.li, 1)
+
+    k0 = rack.index(rank)
+    dests = [rack[(k0 + i) % SET] for i in range(1, SET)] + [rank]
+    n1 = 8 * (2 * 3 - 1)
+    for q in (V, A):
+        q.wait_ge(S.li, 1)
+        q.wait_ge(S.lx2, 16)
+        q.wait_ge(S.arr1, n1)
+    for i, d in enumerate(dests):
+        e = (d + SHIFT) % SET
+        win = T.bl[:, 0:SET * W].indirect(T.offi[:, STR * e:STR * e + W // 16])
+        out = T.rv[:, myhalf * TC + lo:myhalf * TC + hi] if d == rank else T.gt[:, e * W:(e + 1) * W]
+        sem = S.own if d == rank else S["g%d" % i]
+        if i % 2 == 0:
+            V.tensor_copy(out, win).then_inc(sem, 1)
+        else:
+            A.activation(out, win, copy).then_inc(sem, 1)
+
+    for i, d in enumerate(dests[:-1]):
+        e = (d + SHIFT) % SET
+        rid, pid = topo.addr(cores[d], core)
+        g.wait_ge(S["g%d" % i], 1)
+        g.remote_dma(out_ap=T.rv[:, myhalf * TC + lo:myhalf * TC + hi], in_ap=T.gt[:, e * W:(e + 1) * W],
+                     remote_sem=S.arr2, local_sem=S.ls, pid=pid, routing_id=rid,
+                     dma_engine_mask=topo.mask(core, cores[d]))
+
+    step(V.tensor_scalar(T.jj[:], T.jj[:], T.hf[:], None, AluOpType.add))
+    sync_v()
+    step(V.tensor_copy(T.ji[:], T.jj[:]))
+    step(V.tensor_scalar(T.a1[:], T.jj[:], float(6 * TC), float(TC), AluOpType.is_ge, AluOpType.mult))
+    step(V.tensor_scalar(T.a2[:], T.jj[:], float(12 * TC), float(-TC), AluOpType.is_ge, AluOpType.mult))
+    step(V.tensor_scalar(T.a3[:], T.jj[:], float(18 * TC), float(TC), AluOpType.is_ge, AluOpType.mult))
+    sync_v()
+    step(V.tensor_scalar(T.jr[:], T.ji[:], TC - 1, None, AluOpType.bitwise_and))
+    step(V.tensor_tensor(T.a1[:], T.a1[:], T.a2[:], AluOpType.add))
+    sync_v()
+    step(V.tensor_copy(T.jj[:], T.jr[:]))
+    step(V.tensor_tensor(T.a1[:], T.a1[:], T.a3[:], AluOpType.add))
+    sync_v()
+    step(V.tensor_tensor(T.a1[:], T.a1[:], T.jj[:], AluOpType.add))
+    sync_v()
+    V.tensor_copy(T.offf[:], T.a1[:]).then_inc(S.lf, 1)
+
+    n2 = 8 * (SET - 1)
+    for q in (V, A):
+        q.wait_ge(S.lf, 1)
+        q.wait_ge(S.own, 1)
+        q.wait_ge(S.arr2, n2)
+    V.tensor_copy(T.yb[:, 0:256], T.rv[:].indirect(T.offf[:, 0:16])).then_inc(S.f0, 1)
+    V.tensor_copy(T.yb[:, 256:512], T.rv[:].indirect(T.offf[:, 16:32])).then_inc(S.f1, 1)
+    A.activation(T.yb[:, 512:1024], T.rv[:].indirect(T.offf[:, 32:64]), copy).then_inc(S.f2, 1)
+    g.sync.wait_ge(S.f0, 1)
+    g.sync.dma_start(out=T.y[:, 0:256], in_=T.yb[:, 0:256]).then_inc(S.st, 16)
+    g.sync.wait_ge(S.f1, 1)
+    g.sync.dma_start(out=T.y[:, 256:512], in_=T.yb[:, 256:512]).then_inc(S.st, 16)
+    A.wait_ge(S.f2, 1)
+    A.dma_start(out=T.y[:, 512:1024], in_=T.yb[:, 512:1024]).then_inc(S.st, 16)
+    V.wait_ge(S.v, nv[0])
+    g.wait_ge(S.ls, 8 * (3 + SET - 1))
+    g.wait_ge(S.st, 48)

@@ -3,16 +3,15 @@ from concourse.mybir import AluOpType, ActivationFunctionType
 
 NR = 12
 TC = 1024
-SET = 6
-SLICES = [(0, 352), (352, 688), (688, 1024)]
-STR = 22
-SHIFT = 3
+RK = 6
+WH = 96
+W_BIG, W_SMALL = 80, 64
 
 SCRATCH = {
     "xs": ("sbuf", [128, TC], "float32"),
-    "bl": ("sbuf", [128, SET * 352], "float32"),
-    "gt": ("sbuf", [128, SET * 352], "float32"),
-    "rv": ("sbuf", [128, 2 * TC], "float32"),
+    "bl": ("sbuf", [128, NR * WH], "float32"),
+    "gt": ("sbuf", [128, RK * WH], "float32"),
+    "rv": ("sbuf", [128, TC], "float32"),
     "yb": ("sbuf", [128, TC], "float32"),
     "ht": ("sbuf", [16, 2], "int32"),
     "hb": ("sbuf", [128, 2], "int32"),
@@ -20,83 +19,161 @@ SCRATCH = {
     "pf": ("sbuf", [128, 1], "float32"),
     "sq": ("sbuf", [128, 2], "int32"),
     "sf": ("sbuf", [128, 2], "float32"),
-    "hf": ("sbuf", [128, 1], "float32"),
-    "qt": ("sbuf", [128, 1], "float32"),
-    "r6": ("sbuf", [128, SET * STR], "float32"),
-    "ec": ("sbuf", [128, SET * STR], "float32"),
-    "u1": ("sbuf", [128, SET * STR], "float32"),
-    "u2": ("sbuf", [128, SET * STR], "float32"),
+    "qw": ("sbuf", [128, 1], "float32"),
+    "r6": ("sbuf", [128, RK * WH // 16], "float32"),
+    "ec": ("sbuf", [128, RK * WH // 16], "float32"),
+    "u1": ("sbuf", [128, RK * WH // 16], "float32"),
+    "u2": ("sbuf", [128, RK * WH // 16], "float32"),
     "jj": ("sbuf", [128, 64], "float32"),
     "ji": ("sbuf", [128, 64], "int32"),
     "jr": ("sbuf", [128, 64], "int32"),
-    "a1": ("sbuf", [128, 64], "float32"),
-    "a2": ("sbuf", [128, 64], "float32"),
-    "a3": ("sbuf", [128, 64], "float32"),
-    "offi": ("sbuf", [128, SET * STR], "uint16"),
+    "offi": ("sbuf", [128, RK * WH // 16], "uint16"),
+    "offl": ("sbuf", [128, 64], "uint16"),
     "offf": ("sbuf", [128, 64], "uint16"),
 }
-SEMAPHORES = ["lh", "lx0", "lx1", "lx2", "tab", "hb", "v", "li", "lf", "arr1", "arr2", "ls", "own", "f0", "f1", "f2",
-              "st", "g0", "g1", "g2", "g3", "g4"]
+SEMAPHORES = ["lh", "lxa", "lxb", "lxo", "tab", "hb", "v", "li", "lf", "fl", "arr1", "arr2", "arr3", "ls", "gv", "ga", "own",
+              "f0", "f1", "f2", "st"]
 
 
-def half_of(q):
-    return ((q + SHIFT) % NR) // SET
+def bits(mask):
+    return [b for b in range(16) if mask >> b & 1]
+
+
+def to_mask(bs):
+    return sum(1 << b for b in bs)
+
+
+def deal(engines, n):
+    e = len(engines)
+    cut = {1: [e], 2: [e // 2, e // 2], 3: [e // 4, e // 4, e // 2], 4: [e // 4] * 4}[n]
+    out, at = [], 0
+    for c in cut:
+        out.append(to_mask(engines[at:at + c]))
+        at += c
+    return out
+
+
+def layout(T, topo):
+    cores = T.cores
+    ranks = list(range(NR))
+    racks = [[r for r in ranks if topo.rack(topo.host(cores[r])) == k] for k in (0, 1)]
+    side = [0 if r in racks[0] else 1 for r in ranks]
+    partner = [[p for p in ranks if side[p] != side[r] and topo.chip(cores[p]) == topo.chip(cores[r])
+                and topo.may_write(cores[r], cores[p])][0] for r in ranks]
+    label = [racks[0].index(r if side[r] == 0 else partner[r]) for r in ranks]
+    helper = []
+    for r in ranks:
+        c = cores[r]
+        first = c - c % 8
+        helper.append([d for d in range(first, first + 8) if topo.chip(d) == topo.chip(c) and topo.die(d) != topo.die(c)
+                       and all(topo.may_write(d, cores[p]) for p in racks[side[r]])][0])
+    width0 = []
+    for r in racks[0]:
+        kin = [p for p in racks[0] if topo.same_plane(cores[p], cores[r])]
+        width0.append(W_SMALL if len(kin) < 2 else W_BIG)
+    lo0 = [RK * WH + sum(width0[:i]) for i in range(RK)]
+    far = bits(topo.mask(cores[0], cores[1]))
+    near = [b for b in bits(topo.mask(cores[0], helper[0])) if b not in far][:4]
+    return {"cores": cores, "racks": racks, "side": side, "partner": partner, "label": label, "helper": helper,
+            "width0": width0, "lo0": lo0, "far": far, "near": near}
+
+
+def slice_of(L, lane, r):
+    k = L["label"][r]
+    return (k * WH, (k + 1) * WH) if lane else (L["lo0"][k], L["lo0"][k] + L["width0"][k])
+
+
+def peers_of(L, r):
+    rack = L["racks"][L["side"][r]]
+    k = rack.index(r)
+    return [rack[(k + i) % RK] for i in range(1, RK)]
+
+
+def hop1_calls(L, r):
+    peers = peers_of(L, r)
+    first = list(zip(peers[:4], deal(L["far"], 4))) + [(r, to_mask(L["near"]))]
+    calls = [(1, first), (1, [(peers[4], to_mask(L["far"]))])]
+    for w in (W_BIG, W_SMALL):
+        grp = [p for p in peers if L["width0"][L["label"][p]] == w]
+        calls.append((0, list(zip(grp, deal(L["far"], len(grp))))))
+    return calls
+
+
+def hop3_calls(L, lane, r):
+    peers = peers_of(L, r)
+    first = list(zip(peers[:4], deal(L["far"], 4)))
+    if lane:
+        first.append((r, to_mask(L["near"])))
+    return [first, [(peers[4], to_mask(L["far"]))]]
+
+
+def arrivals(calls, r):
+    return sum(len(bits(mk)) for call in calls for d, mk in call if d == r)
 
 
 def rank_program(g, core, T, topo):
-    rank = T.rank_of(core)
-    if rank is None:
+    L = layout(T, topo)
+    cores = L["cores"]
+    if core in cores:
+        lane, rank = 0, cores.index(core)
+    elif core in L["helper"]:
+        lane, rank = 1, L["helper"].index(core)
+    else:
         return
     S = T.sem
     V, A = g.vector, g.scalar
-    cores = T.cores
     copy = ActivationFunctionType.Copy
-    ranks = list(range(NR))
-    own = [r for r in ranks if topo.host(cores[r]) == topo.host(core)]
-    rack = [r for r in ranks if topo.rack(topo.host(cores[r])) == topo.rack(topo.host(core))]
-    cabled = [r for r in ranks if r not in rack and topo.may_write(core, cores[r])]
-    m = own.index(rank)
-    lo, hi = SLICES[m]
+    rack = L["racks"][L["side"][rank]]
+    home = cores[rank]
+    helper = L["helper"][rank]
+    where = [[cores[r] for r in range(NR)], L["helper"]]
+    lo, hi = slice_of(L, lane, rank)
     W = hi - lo
-    place = (rank + SHIFT) % SET
-    myhalf = half_of(rank)
+    n = W // 16
+    sent = [0]
 
-    order = [(m + 1) % 3, (m + 2) % 3, m]
-    srcs = []
-    for mm in order:
-        a, b = SLICES[mm]
-        srcs.append(T.bl[:, place * W:(place + 1) * W] if mm == m else T.xs[:, a:b])
-    a, b = SLICES[order[0]]
-    g.sync.dma_start(out=srcs[0], in_=T.x[:, a:b]).then_inc(S.lx0, 16)
-    a, b = SLICES[order[1]]
-    A.dma_start(out=srcs[1], in_=T.x[:, a:b]).then_inc(S.lx1, 16)
-    a, b = SLICES[order[2]]
-    g.sync.dma_start(out=srcs[2], in_=T.x[:, a:b]).then_inc(S.lx2, 16)
-    A.dma_start(out=T.ht[:], in_=T.hh[:]).then_inc(S.lh, 16)
+    def fused(items):
+        ts = []
+        for dst, mk, sem, src, out in items:
+            rid, pid = topo.addr(dst, core)
+            ts.append(RemoteDMATransfer(dst_ids=[DstId(rid=rid, pnc=pid)], dma_engine_mask=mk, remote_sem=sem,
+                                        srcs=[src], dsts=[out]))
+            sent[0] += len(bits(mk))
+        g.remote_dma_fused(ts, local_sem=S.ls)
 
-    base = (TC * rank + SHIFT * TC) % (NR * TC)
+    if lane == 0:
+        h1, h2, c1 = RK * WH // 2, RK * WH, (RK * WH + TC) // 2
+        g.sync.dma_start(out=T.ht[:], in_=T.hh[:]).then_inc(S.lh, 16)
+        A.dma_start(out=T.xs[:, 0:h1], in_=T.x[:, 0:h1]).then_inc(S.lxa, 16)
+        g.sync.dma_start(out=T.xs[:, h1:h2], in_=T.x[:, h1:h2]).then_inc(S.lxa, 16)
+        A.dma_start(out=T.xs[:, h2:c1], in_=T.x[:, h2:c1]).then_inc(S.lxb, 16)
+        g.sync.dma_start(out=T.xs[:, c1:TC], in_=T.x[:, c1:TC]).then_inc(S.lxb, 16)
+        A.dma_start(out=T.bl[:, rank * W:(rank + 1) * W], in_=T.x[:, lo:hi]).then_inc(S.lxo, 16)
+
     g.iota(T.pi[:], [[0, 1]], 0, 1).then_inc(S.tab, 1)
-    g.iota(T.r6[:], [[0, SET], [16, STR]], lo, 0, allow_small_or_imprecise_dtypes=True).then_inc(S.tab, 1)
-    g.iota(T.ec[:], [[W, SET], [16, STR]], 0, 0, allow_small_or_imprecise_dtypes=True).then_inc(S.tab, 1)
-    g.iota(T.jj[:], [[16, 64]], base, 0, allow_small_or_imprecise_dtypes=True).then_inc(S.tab, 1)
+    g.iota(T.r6[:, 0:RK * n], [[0, RK], [16, n]], lo, 0, allow_small_or_imprecise_dtypes=True).then_inc(S.tab, 1)
+    g.iota(T.ec[:, 0:RK * n], [[W, RK], [16, n]], W * rack[0], 0, allow_small_or_imprecise_dtypes=True).then_inc(S.tab, 1)
+    if lane == 1:
+        g.iota(T.jj[:], [[16, 64]], 0, 0, allow_small_or_imprecise_dtypes=True).then_inc(S.tab, 1)
 
-    for k, mm in enumerate(order):
-        ma, mb = SLICES[mm]
-        mw = mb - ma
-        peers = [grp[mm] for grp in (cabled, own) if grp[mm] != rank]
-        ids, dsts, mask = [], [], None
-        for r in peers:
-            rid, pid = topo.addr(cores[r], core)
-            ids.append(DstId(rid=rid, pnc=pid))
-            dsts.append(T.bl[:, place * mw:(place + 1) * mw])
-            mk = topo.mask(core, cores[r])
-            mask = mk if mask is None else mask & mk
-        g.wait_ge(S["lx%d" % k], 16)
-        g.remote_dma_fused([RemoteDMATransfer(dst_ids=ids, dma_engine_mask=mask, remote_sem=S.arr1,
-                                              srcs=[srcs[k]], dsts=dsts)], local_sem=S.ls)
+    if lane == 0:
+        g.wait_ge(S.lh, 16)
+        g.partition_broadcast(T.hb[:], T.ht[0:1, :], 128).then_inc(S.hb, 1)
+        g.wait_ge(S.hb, 1)
+        fused([(helper, to_mask(L["far"]), S.hb, T.hb[:], T.hb[:])])
+    hb_in = 1 if lane == 0 else len(L["far"])
 
-    g.wait_ge(S.lh, 16)
-    g.partition_broadcast(T.hb[:], T.ht[0:1, :], 128).then_inc(S.hb, 1)
+    if lane == 0:
+        for i, (ln, call) in enumerate(hop1_calls(L, rank)):
+            if i == 0:
+                g.wait_ge(S.lxa, 32)
+            if i == 2:
+                g.wait_ge(S.lxb, 32)
+            items = []
+            for d, mk in call:
+                a, b = slice_of(L, ln, d)
+                items.append((where[ln][d], mk, S.arr1, T.xs[:, a:b], T.bl[:, rank * (b - a):(rank + 1) * (b - a)]))
+            fused(items)
 
     nv = [0]
 
@@ -107,92 +184,83 @@ def rank_program(g, core, T, topo):
     def sync_v():
         V.wait_ge(S.v, nv[0])
 
-    V.wait_ge(S.tab, 4)
+    r6, ec, u1, u2 = (t[:, 0:RK * n] for t in (T.r6, T.ec, T.u1, T.u2))
+    V.wait_ge(S.tab, 3 + lane)
     step(V.tensor_scalar(T.pi[:], T.pi[:], 15, None, AluOpType.bitwise_and))
     sync_v()
     step(V.tensor_copy(T.pf[:], T.pi[:]))
     sync_v()
-    for t in (T.r6, T.ec, T.jj):
-        step(V.tensor_scalar(t[:], t[:], T.pf[:], None, AluOpType.add))
-    V.wait_ge(S.hb, 1)
+    step(V.tensor_scalar(r6, r6, T.pf[:], None, AluOpType.add))
+    V.wait_ge(S.hb, hb_in)
     step(V.tensor_scalar(T.sq[:, 0:1], T.hb[:, 0:1], TC - 1, None, AluOpType.bitwise_and))
     step(V.tensor_scalar(T.sq[:, 1:2], T.hb[:, 0:1], 10, None, AluOpType.logical_shift_right))
-    step(V.tensor_copy(T.hf[:], T.hb[:, 0:1]))
     sync_v()
     step(V.tensor_copy(T.sf[:], T.sq[:]))
     sync_v()
-    step(V.tensor_scalar(T.qt[:], T.sf[:, 1:2], float(SET), float(-SET), AluOpType.is_ge, AluOpType.mult))
+    if lane == 1:
+        step(V.tensor_scalar(T.ji[:], T.jj[:], T.pf[:], T.sf[:, 0:1], AluOpType.add, AluOpType.add))
+        sync_v()
+        step(V.tensor_scalar(T.jr[:], T.ji[:], TC - 1, None, AluOpType.bitwise_and))
+        sync_v()
+        V.tensor_copy(T.offl[:], T.jr[:]).then_inc(S.fl, 1)
+        g.wait_ge(S.fl, 1)
+        fused([(home, to_mask(L["far"]), S.lf, T.offl[:], T.offf[:])])
+    step(V.tensor_scalar(T.qw[:], T.sf[:, 1:2], float(W), None, AluOpType.mult))
+    step(V.tensor_scalar(u1, r6, T.sf[:, 0:1], float(W), AluOpType.is_lt, AluOpType.mult))
     sync_v()
-    step(V.tensor_tensor(T.qt[:], T.qt[:], T.sf[:, 1:2], AluOpType.add))
+    step(V.tensor_scalar(ec, ec, T.pf[:], T.qw[:], AluOpType.add, AluOpType.add))
     sync_v()
-    step(V.tensor_scalar(T.u1[:], T.r6[:], T.sf[:, 0:1], T.qt[:], AluOpType.is_lt, AluOpType.add))
+    step(V.tensor_tensor(u1, u1, ec, AluOpType.add))
     sync_v()
-    step(V.tensor_scalar(T.u1[:], T.u1[:], float(W), None, AluOpType.mult))
+    step(V.tensor_scalar(u2, u1, float(NR * W), float(-NR * W), AluOpType.is_ge, AluOpType.mult))
     sync_v()
-    step(V.tensor_tensor(T.u1[:], T.u1[:], T.ec[:], AluOpType.add))
+    step(V.tensor_tensor(u1, u1, u2, AluOpType.add))
     sync_v()
-    step(V.tensor_scalar(T.u2[:], T.u1[:], float(SET * W), float(-SET * W), AluOpType.is_ge, AluOpType.mult))
-    sync_v()
-    step(V.tensor_tensor(T.u1[:], T.u1[:], T.u2[:], AluOpType.add))
-    sync_v()
-    V.tensor_copy(T.offi[:], T.u1[:]).then_inc(S.li, 1)
+    V.tensor_copy(T.offi[:, 0:RK * n], u1).then_inc(S.li, 1)
 
-    k0 = rack.index(rank)
-    dests = [rack[(k0 + i) % SET] for i in range(1, SET)] + [rank]
-    n1 = 8 * (2 * 3 - 1)
+    n1 = sum(arrivals([c for ln, c in hop1_calls(L, r) if ln == lane], rank) for r in rack)
+    g.wait_ge(S.arr1, n1)
+    if lane == 0:
+        g.wait_ge(S.lxo, 16)
+    six = T.bl[:, rack[0] * W:(rack[-1] + 1) * W]
+    fused([(where[lane][L["partner"][rank]], to_mask(L["far"]), S.arr2, six, six)])
+
+    cut = 3 if (3 * n) % 2 == 0 else 4
+    win = T.bl[:, 0:NR * W]
     for q in (V, A):
         q.wait_ge(S.li, 1)
-        q.wait_ge(S.lx2, 16)
         q.wait_ge(S.arr1, n1)
-    for i, d in enumerate(dests):
-        e = (d + SHIFT) % SET
-        win = T.bl[:, 0:SET * W].indirect(T.offi[:, STR * e:STR * e + W // 16])
-        out = T.rv[:, myhalf * TC + lo:myhalf * TC + hi] if d == rank else T.gt[:, e * W:(e + 1) * W]
-        sem = S.own if d == rank else S["g%d" % i]
-        if i % 2 == 0:
-            V.tensor_copy(out, win).then_inc(sem, 1)
-        else:
-            A.activation(out, win, copy).then_inc(sem, 1)
+        if lane == 0:
+            q.wait_ge(S.lxo, 16)
+        q.wait_ge(S.arr2, len(L["far"]))
+    V.tensor_copy(T.gt[:, 0:cut * W], win.indirect(T.offi[:, 0:cut * n])).then_inc(S.gv, 1)
+    A.activation(T.gt[:, cut * W:RK * W], win.indirect(T.offi[:, cut * n:RK * n]), copy).then_inc(S.ga, 1)
 
-    for i, d in enumerate(dests[:-1]):
-        e = (d + SHIFT) % SET
-        rid, pid = topo.addr(cores[d], core)
-        g.wait_ge(S["g%d" % i], 1)
-        g.remote_dma(out_ap=T.rv[:, myhalf * TC + lo:myhalf * TC + hi], in_ap=T.gt[:, e * W:(e + 1) * W],
-                     remote_sem=S.arr2, local_sem=S.ls, pid=pid, routing_id=rid,
-                     dma_engine_mask=topo.mask(core, cores[d]))
+    g.wait_ge(S.gv, 1)
+    g.wait_ge(S.ga, 1)
+    for call in hop3_calls(L, lane, rank):
+        fused([(cores[d], mk, S.arr3, T.gt[:, rack.index(d) * W:(rack.index(d) + 1) * W], T.rv[:, lo:hi]) for d, mk in call])
 
-    step(V.tensor_scalar(T.jj[:], T.jj[:], T.hf[:], None, AluOpType.add))
-    sync_v()
-    step(V.tensor_copy(T.ji[:], T.jj[:]))
-    step(V.tensor_scalar(T.a1[:], T.jj[:], float(6 * TC), float(TC), AluOpType.is_ge, AluOpType.mult))
-    step(V.tensor_scalar(T.a2[:], T.jj[:], float(12 * TC), float(-TC), AluOpType.is_ge, AluOpType.mult))
-    step(V.tensor_scalar(T.a3[:], T.jj[:], float(18 * TC), float(TC), AluOpType.is_ge, AluOpType.mult))
-    sync_v()
-    step(V.tensor_scalar(T.jr[:], T.ji[:], TC - 1, None, AluOpType.bitwise_and))
-    step(V.tensor_tensor(T.a1[:], T.a1[:], T.a2[:], AluOpType.add))
-    sync_v()
-    step(V.tensor_copy(T.jj[:], T.jr[:]))
-    step(V.tensor_tensor(T.a1[:], T.a1[:], T.a3[:], AluOpType.add))
-    sync_v()
-    step(V.tensor_tensor(T.a1[:], T.a1[:], T.jj[:], AluOpType.add))
-    sync_v()
-    V.tensor_copy(T.offf[:], T.a1[:]).then_inc(S.lf, 1)
-
-    n2 = 8 * (SET - 1)
-    for q in (V, A):
-        q.wait_ge(S.lf, 1)
-        q.wait_ge(S.own, 1)
-        q.wait_ge(S.arr2, n2)
-    V.tensor_copy(T.yb[:, 0:256], T.rv[:].indirect(T.offf[:, 0:16])).then_inc(S.f0, 1)
-    V.tensor_copy(T.yb[:, 256:512], T.rv[:].indirect(T.offf[:, 16:32])).then_inc(S.f1, 1)
-    A.activation(T.yb[:, 512:1024], T.rv[:].indirect(T.offf[:, 32:64]), copy).then_inc(S.f2, 1)
-    g.sync.wait_ge(S.f0, 1)
-    g.sync.dma_start(out=T.y[:, 0:256], in_=T.yb[:, 0:256]).then_inc(S.st, 16)
-    g.sync.wait_ge(S.f1, 1)
-    g.sync.dma_start(out=T.y[:, 256:512], in_=T.yb[:, 256:512]).then_inc(S.st, 16)
-    A.wait_ge(S.f2, 1)
-    A.dma_start(out=T.y[:, 512:1024], in_=T.yb[:, 512:1024]).then_inc(S.st, 16)
+    if lane == 0:
+        k = rack.index(rank)
+        V.wait_ge(S.gv, 1)
+        V.wait_ge(S.ga, 1)
+        V.tensor_copy(T.rv[:, lo:hi], T.gt[:, k * W:(k + 1) * W]).then_inc(S.own, 1)
+        n3 = sum(arrivals(hop3_calls(L, ln, r), rank) for r in rack for ln in (0, 1))
+        for q in (V, A):
+            q.wait_ge(S.lf, len(L["far"]))
+            q.wait_ge(S.own, 1)
+            q.wait_ge(S.arr3, n3)
+        V.tensor_copy(T.yb[:, 0:256], T.rv[:].indirect(T.offf[:, 0:16])).then_inc(S.f0, 1)
+        V.tensor_copy(T.yb[:, 256:512], T.rv[:].indirect(T.offf[:, 16:32])).then_inc(S.f1, 1)
+        A.activation(T.yb[:, 512:1024], T.rv[:].indirect(T.offf[:, 32:64]), copy).then_inc(S.f2, 1)
+        g.sync.wait_ge(S.f0, 1)
+        g.sync.dma_start(out=T.y[:, 0:256], in_=T.yb[:, 0:256]).then_inc(S.st, 16)
+        g.sync.wait_ge(S.f1, 1)
+        g.sync.dma_start(out=T.y[:, 256:512], in_=T.yb[:, 256:512]).then_inc(S.st, 16)
+        A.wait_ge(S.f2, 1)
+        A.dma_start(out=T.y[:, 512:1024], in_=T.yb[:, 512:1024]).then_inc(S.st, 16)
     V.wait_ge(S.v, nv[0])
-    g.wait_ge(S.ls, 8 * (3 + SET - 1))
-    g.wait_ge(S.st, 48)
+    g.wait_ge(S.ls, sent[0])
+    if lane == 0:
+        g.wait_ge(S.st, 48)

@@ -4,35 +4,37 @@ from concourse.mybir import AluOpType, ActivationFunctionType
 NR = 12
 TC = 1024
 RK = 6
-WH = 96
-W_BIG, W_SMALL = 80, 64
+WH = 88
+W_BIG, W_SMALL = 84, 80
+PAD = 96
 
 SCRATCH = {
     "xs": ("sbuf", [128, TC], "float32"),
     "bl": ("sbuf", [128, NR * WH], "float32"),
-    "gt": ("sbuf", [128, RK * WH], "float32"),
+    "gt": ("sbuf", [128, RK * PAD], "float32"),
     "rv": ("sbuf", [128, TC], "float32"),
     "yb": ("sbuf", [128, TC], "float32"),
     "ht": ("sbuf", [16, 2], "int32"),
     "hb": ("sbuf", [128, 2], "int32"),
     "pi": ("sbuf", [128, 1], "int32"),
     "pf": ("sbuf", [128, 1], "float32"),
+    "hf": ("sbuf", [128, 1], "float32"),
     "sq": ("sbuf", [128, 2], "int32"),
     "sf": ("sbuf", [128, 2], "float32"),
-    "qw": ("sbuf", [128, 1], "float32"),
-    "r6": ("sbuf", [128, RK * WH // 16], "float32"),
-    "ec": ("sbuf", [128, RK * WH // 16], "float32"),
-    "u1": ("sbuf", [128, RK * WH // 16], "float32"),
-    "u2": ("sbuf", [128, RK * WH // 16], "float32"),
+    "r6": ("sbuf", [128, RK * PAD // 16], "float32"),
+    "dd": ("sbuf", [128, RK * PAD // 16], "float32"),
+    "u1": ("sbuf", [128, RK * PAD // 16], "float32"),
+    "u2": ("sbuf", [128, RK * PAD // 16], "float32"),
+    "u3": ("sbuf", [128, RK * PAD // 16], "float32"),
     "jj": ("sbuf", [128, 64], "float32"),
     "ji": ("sbuf", [128, 64], "int32"),
     "jr": ("sbuf", [128, 64], "int32"),
-    "offi": ("sbuf", [128, RK * WH // 16], "uint16"),
+    "offi": ("sbuf", [128, RK * PAD // 16], "uint16"),
     "offl": ("sbuf", [128, 64], "uint16"),
     "offf": ("sbuf", [128, 64], "uint16"),
 }
-SEMAPHORES = ["lh", "lxa", "lxb", "lxo", "tab", "hb", "v", "li", "lf", "fl", "arr1", "arr2", "arr3", "ls", "gv", "ga", "own",
-              "f0", "f1", "f2", "st"]
+SEMAPHORES = ["lh", "lxr", "lxa", "lxb", "lxo", "tab", "hb", "v", "li", "lf", "fl", "arrr", "arr1", "arr2", "arr3", "ls", "gv",
+              "ga", "own", "f0", "f1", "f2", "st"]
 
 
 def bits(mask):
@@ -72,15 +74,28 @@ def layout(T, topo):
         kin = [p for p in racks[0] if topo.same_plane(cores[p], cores[r])]
         width0.append(W_SMALL if len(kin) < 2 else W_BIG)
     lo0 = [RK * WH + sum(width0[:i]) for i in range(RK)]
+    near_host = [[p for p in racks[side[r]] if topo.host(cores[p]) == topo.host(cores[r])] for r in ranks]
+    far_host = [[p for p in racks[side[r]] if topo.host(cores[p]) != topo.host(cores[r])] for r in ranks]
     far = bits(topo.mask(cores[0], cores[1]))
-    near = [b for b in bits(topo.mask(cores[0], helper[0])) if b not in far][:4]
+    near = [b for b in bits(topo.mask(cores[0], helper[0])) if b not in far][::2]
     return {"cores": cores, "racks": racks, "side": side, "partner": partner, "label": label, "helper": helper,
-            "width0": width0, "lo0": lo0, "far": far, "near": near}
+            "width0": width0, "lo0": lo0, "far": far, "near": near, "near_host": near_host, "far_host": far_host}
 
 
 def slice_of(L, lane, r):
     k = L["label"][r]
     return (k * WH, (k + 1) * WH) if lane else (L["lo0"][k], L["lo0"][k] + L["width0"][k])
+
+
+def span_of(L, group):
+    ks = [L["label"][r] for r in group]
+    return min(ks) * WH, (max(ks) + 1) * WH
+
+
+def place_of(L, q, r):
+    s = L["side"][q]
+    mine = r if L["side"][r] == s else L["partner"][r]
+    return RK * s + (q - mine - 1) % RK
 
 
 def peers_of(L, r):
@@ -91,12 +106,17 @@ def peers_of(L, r):
 
 def hop1_calls(L, r):
     peers = peers_of(L, r)
-    first = list(zip(peers[:4], deal(L["far"], 4))) + [(r, to_mask(L["near"]))]
-    calls = [(1, first), (1, [(peers[4], to_mask(L["far"]))])]
+    grp = [p for p in peers if p in L["near_host"][r]] + [L["partner"][r], r]
+    calls = [(1, list(zip(grp, deal(L["far"], len(grp)))))]
     for w in (W_BIG, W_SMALL):
-        grp = [p for p in peers if L["width0"][L["label"][p]] == w]
+        grp = [p for p in peers + [L["partner"][r]] if L["width0"][L["label"][p]] == w]
         calls.append((0, list(zip(grp, deal(L["far"], len(grp))))))
     return calls
+
+
+def relay_calls(L, r):
+    grp = [p for p in peers_of(L, r) if p in L["far_host"][r]]
+    return [(1, list(zip(grp, deal(L["far"], len(grp)))))]
 
 
 def hop3_calls(L, lane, r):
@@ -123,13 +143,16 @@ def rank_program(g, core, T, topo):
     S = T.sem
     V, A = g.vector, g.scalar
     copy = ActivationFunctionType.Copy
-    rack = L["racks"][L["side"][rank]]
+    side = L["side"][rank]
+    rack = L["racks"][side]
+    pal = L["partner"][rank]
     home = cores[rank]
     helper = L["helper"][rank]
     where = [[cores[r] for r in range(NR)], L["helper"]]
     lo, hi = slice_of(L, lane, rank)
     W = hi - lo
-    n = W // 16
+    n = (W + 15) // 16
+    PW = 16 * n
     sent = [0]
 
     def fused(items):
@@ -141,39 +164,45 @@ def rank_program(g, core, T, topo):
             sent[0] += len(bits(mk))
         g.remote_dma_fused(ts, local_sem=S.ls)
 
+    def slices(calls, before):
+        for i, (ln, call) in enumerate(calls):
+            if i in before:
+                g.wait_ge(*before[i])
+            items = []
+            for d, mk in call:
+                a, b = slice_of(L, ln, d)
+                p = place_of(L, rank, d)
+                items.append((where[ln][d], mk, S.arr2 if d == pal else S.arr1, T.xs[:, a:b],
+                              T.bl[:, p * (b - a):(p + 1) * (b - a)]))
+            fused(items)
+
+    ra, rb = span_of(L, L["far_host"][rank])
     if lane == 0:
-        h1, h2, c1 = RK * WH // 2, RK * WH, (RK * WH + TC) // 2
+        na, nb = span_of(L, L["near_host"][rank])
+        h2, c1 = RK * WH, (RK * WH + TC) // 2
+        p = place_of(L, rank, rank)
         g.sync.dma_start(out=T.ht[:], in_=T.hh[:]).then_inc(S.lh, 16)
-        A.dma_start(out=T.xs[:, 0:h1], in_=T.x[:, 0:h1]).then_inc(S.lxa, 16)
-        g.sync.dma_start(out=T.xs[:, h1:h2], in_=T.x[:, h1:h2]).then_inc(S.lxa, 16)
+        A.dma_start(out=T.xs[:, ra:rb], in_=T.x[:, ra:rb]).then_inc(S.lxr, 16)
+        g.sync.dma_start(out=T.xs[:, na:nb], in_=T.x[:, na:nb]).then_inc(S.lxa, 16)
         A.dma_start(out=T.xs[:, h2:c1], in_=T.x[:, h2:c1]).then_inc(S.lxb, 16)
         g.sync.dma_start(out=T.xs[:, c1:TC], in_=T.x[:, c1:TC]).then_inc(S.lxb, 16)
-        A.dma_start(out=T.bl[:, rank * W:(rank + 1) * W], in_=T.x[:, lo:hi]).then_inc(S.lxo, 16)
+        A.dma_start(out=T.bl[:, p * W:(p + 1) * W], in_=T.x[:, lo:hi]).then_inc(S.lxo, 16)
 
     g.iota(T.pi[:], [[0, 1]], 0, 1).then_inc(S.tab, 1)
-    g.iota(T.r6[:, 0:RK * n], [[0, RK], [16, n]], lo, 0, allow_small_or_imprecise_dtypes=True).then_inc(S.tab, 1)
-    g.iota(T.ec[:, 0:RK * n], [[W, RK], [16, n]], W * rack[0], 0, allow_small_or_imprecise_dtypes=True).then_inc(S.tab, 1)
     if lane == 1:
         g.iota(T.jj[:], [[16, 64]], 0, 0, allow_small_or_imprecise_dtypes=True).then_inc(S.tab, 1)
+    g.iota(T.r6[:, 0:RK * n], [[0, RK], [16, n]], lo, 0, allow_small_or_imprecise_dtypes=True).then_inc(S.tab, 1)
+    g.iota(T.dd[:, 0:RK * n], [[1, RK], [0, n]], rack[0], 0, allow_small_or_imprecise_dtypes=True).then_inc(S.tab, 1)
 
     if lane == 0:
         g.wait_ge(S.lh, 16)
         g.partition_broadcast(T.hb[:], T.ht[0:1, :], 128).then_inc(S.hb, 1)
         g.wait_ge(S.hb, 1)
         fused([(helper, to_mask(L["far"]), S.hb, T.hb[:], T.hb[:])])
+        g.wait_ge(S.lxr, 16)
+        fused([(helper, to_mask(L["near"]), S.arrr, T.xs[:, ra:rb], T.xs[:, ra:rb])])
+        slices(hop1_calls(L, rank), {0: (S.lxa, 16), 1: (S.lxb, 32)})
     hb_in = 1 if lane == 0 else len(L["far"])
-
-    if lane == 0:
-        for i, (ln, call) in enumerate(hop1_calls(L, rank)):
-            if i == 0:
-                g.wait_ge(S.lxa, 32)
-            if i == 2:
-                g.wait_ge(S.lxb, 32)
-            items = []
-            for d, mk in call:
-                a, b = slice_of(L, ln, d)
-                items.append((where[ln][d], mk, S.arr1, T.xs[:, a:b], T.bl[:, rank * (b - a):(rank + 1) * (b - a)]))
-            fused(items)
 
     nv = [0]
 
@@ -184,7 +213,7 @@ def rank_program(g, core, T, topo):
     def sync_v():
         V.wait_ge(S.v, nv[0])
 
-    r6, ec, u1, u2 = (t[:, 0:RK * n] for t in (T.r6, T.ec, T.u1, T.u2))
+    r6, dd, u1, u2, u3 = (t[:, 0:RK * n] for t in (T.r6, T.dd, T.u1, T.u2, T.u3))
     V.wait_ge(S.tab, 3 + lane)
     step(V.tensor_scalar(T.pi[:], T.pi[:], 15, None, AluOpType.bitwise_and))
     sync_v()
@@ -192,38 +221,59 @@ def rank_program(g, core, T, topo):
     sync_v()
     step(V.tensor_scalar(r6, r6, T.pf[:], None, AluOpType.add))
     V.wait_ge(S.hb, hb_in)
-    step(V.tensor_scalar(T.sq[:, 0:1], T.hb[:, 0:1], TC - 1, None, AluOpType.bitwise_and))
-    step(V.tensor_scalar(T.sq[:, 1:2], T.hb[:, 0:1], 10, None, AluOpType.logical_shift_right))
-    sync_v()
-    step(V.tensor_copy(T.sf[:], T.sq[:]))
-    sync_v()
     if lane == 1:
-        step(V.tensor_scalar(T.ji[:], T.jj[:], T.pf[:], T.sf[:, 0:1], AluOpType.add, AluOpType.add))
+        step(V.tensor_copy(T.hf[:], T.hb[:, 0:1]))
+        sync_v()
+        step(V.tensor_scalar(T.ji[:], T.jj[:], T.pf[:], T.hf[:], AluOpType.add, AluOpType.add))
         sync_v()
         step(V.tensor_scalar(T.jr[:], T.ji[:], TC - 1, None, AluOpType.bitwise_and))
         sync_v()
         V.tensor_copy(T.offl[:], T.jr[:]).then_inc(S.fl, 1)
         g.wait_ge(S.fl, 1)
         fused([(home, to_mask(L["far"]), S.lf, T.offl[:], T.offf[:])])
-    step(V.tensor_scalar(T.qw[:], T.sf[:, 1:2], float(W), None, AluOpType.mult))
-    step(V.tensor_scalar(u1, r6, T.sf[:, 0:1], float(W), AluOpType.is_lt, AluOpType.mult))
+        g.wait_ge(S.arrr, len(L["near"]))
+        slices(relay_calls(L, rank), {})
+    step(V.tensor_scalar(T.sq[:, 0:1], T.hb[:, 0:1], TC - 1, None, AluOpType.bitwise_and))
+    step(V.tensor_scalar(T.sq[:, 1:2], T.hb[:, 0:1], 10, None, AluOpType.logical_shift_right))
     sync_v()
-    step(V.tensor_scalar(ec, ec, T.pf[:], T.qw[:], AluOpType.add, AluOpType.add))
+    step(V.tensor_copy(T.sf[:], T.sq[:]))
     sync_v()
-    step(V.tensor_tensor(u1, u1, ec, AluOpType.add))
+    step(V.tensor_scalar(u1, r6, T.sf[:, 0:1], T.sf[:, 1:2], AluOpType.is_lt, AluOpType.add))
     sync_v()
-    step(V.tensor_scalar(u2, u1, float(NR * W), float(-NR * W), AluOpType.is_ge, AluOpType.mult))
+    step(V.tensor_tensor(u1, u1, dd, AluOpType.add))
+    sync_v()
+    step(V.tensor_scalar(u2, u1, float(NR), float(-NR), AluOpType.is_ge, AluOpType.mult))
     sync_v()
     step(V.tensor_tensor(u1, u1, u2, AluOpType.add))
     sync_v()
-    V.tensor_copy(T.offi[:, 0:RK * n], u1).then_inc(S.li, 1)
+    mine = [rank if side == k else pal for k in (0, 1)]
+    a0, a1 = (mine[k] - L["racks"][k][0] + 1 for k in (0, 1))
+    step(V.tensor_scalar(u2, u1, float(RK), float(-(a1 - a0 + RK)), AluOpType.is_ge, AluOpType.mult))
+    step(V.tensor_scalar(u3, u1, float(RK), float(RK), AluOpType.is_ge, AluOpType.mult))
+    sync_v()
+    step(V.tensor_tensor(u1, u1, u2, AluOpType.add))
+    sync_v()
+    step(V.tensor_scalar(u2, u1, float(a0), float(RK), AluOpType.is_lt, AluOpType.mult))
+    step(V.tensor_tensor(u1, u1, u3, AluOpType.add))
+    sync_v()
+    step(V.tensor_tensor(u1, u1, u2, AluOpType.add))
+    sync_v()
+    step(V.tensor_scalar(u1, u1, float(W), None, AluOpType.mult))
+    sync_v()
+    step(V.tensor_tensor(u1, u1, r6, AluOpType.add))
+    sync_v()
+    V.tensor_scalar(T.offi[:, 0:RK * n], u1, float(-(lo + W * a0)), float(NR * W - 1), AluOpType.add,
+                    AluOpType.min).then_inc(S.li, 1)
 
-    n1 = sum(arrivals([c for ln, c in hop1_calls(L, r) if ln == lane], rank) for r in rack)
-    g.wait_ge(S.arr1, n1)
     if lane == 0:
-        g.wait_ge(S.lxo, 16)
-    six = T.bl[:, rack[0] * W:(rack[-1] + 1) * W]
-    fused([(where[lane][L["partner"][rank]], to_mask(L["far"]), S.arr2, six, six)])
+        n1 = sum(arrivals([c for ln, c in hop1_calls(L, r) if ln == 0], rank) for r in rack)
+    else:
+        n1 = sum(arrivals([c for ln, c in hop1_calls(L, r) if ln == 1] + [c for ln, c in relay_calls(L, r)], rank)
+                 for r in rack)
+    n2 = len(L["far"]) + arrivals([c for ln, c in hop1_calls(L, pal) if ln == lane], rank)
+    g.wait_ge(S.arr1, n1)
+    five = T.bl[:, RK * side * W:(RK * side + RK - 1) * W]
+    fused([(where[lane][pal], to_mask(L["far"]), S.arr2, five, five)])
 
     cut = 3 if (3 * n) % 2 == 0 else 4
     win = T.bl[:, 0:NR * W]
@@ -232,20 +282,20 @@ def rank_program(g, core, T, topo):
         q.wait_ge(S.arr1, n1)
         if lane == 0:
             q.wait_ge(S.lxo, 16)
-        q.wait_ge(S.arr2, len(L["far"]))
-    V.tensor_copy(T.gt[:, 0:cut * W], win.indirect(T.offi[:, 0:cut * n])).then_inc(S.gv, 1)
-    A.activation(T.gt[:, cut * W:RK * W], win.indirect(T.offi[:, cut * n:RK * n]), copy).then_inc(S.ga, 1)
+        q.wait_ge(S.arr2, n2)
+    V.tensor_copy(T.gt[:, 0:cut * PW], win.indirect(T.offi[:, 0:cut * n])).then_inc(S.gv, 1)
+    A.activation(T.gt[:, cut * PW:RK * PW], win.indirect(T.offi[:, cut * n:RK * n]), copy).then_inc(S.ga, 1)
 
     g.wait_ge(S.gv, 1)
     g.wait_ge(S.ga, 1)
     for call in hop3_calls(L, lane, rank):
-        fused([(cores[d], mk, S.arr3, T.gt[:, rack.index(d) * W:(rack.index(d) + 1) * W], T.rv[:, lo:hi]) for d, mk in call])
+        fused([(cores[d], mk, S.arr3, T.gt[:, rack.index(d) * PW:rack.index(d) * PW + W], T.rv[:, lo:hi]) for d, mk in call])
 
     if lane == 0:
         k = rack.index(rank)
         V.wait_ge(S.gv, 1)
         V.wait_ge(S.ga, 1)
-        V.tensor_copy(T.rv[:, lo:hi], T.gt[:, k * W:(k + 1) * W]).then_inc(S.own, 1)
+        V.tensor_copy(T.rv[:, lo:hi], T.gt[:, k * PW:k * PW + W]).then_inc(S.own, 1)
         n3 = sum(arrivals(hop3_calls(L, ln, r), rank) for r in rack for ln in (0, 1))
         for q in (V, A):
             q.wait_ge(S.lf, len(L["far"]))

@@ -4,16 +4,24 @@ from concourse.mybir import AluOpType, ActivationFunctionType
 NR = 12
 TC = 1024
 RK = 6
-WH = 88
-W_BIG, W_SMALL = 84, 80
-PAD = 96
+HR = 3
+W = 86
+n = 6
+PW = 16 * n
+GW = HR * W
+GC = 17
+GP = 16 * GC
+GO = 18
+CUT = 10
+NT = NR + 15
 
 SCRATCH = {
     "xs": ("sbuf", [128, TC], "float32"),
-    "bl": ("sbuf", [128, NR * WH], "float32"),
-    "gt": ("sbuf", [128, RK * PAD], "float32"),
-    "rv": ("sbuf", [128, TC], "float32"),
-    "yb": ("sbuf", [128, TC], "float32"),
+    "gs": ("sbuf", [128, 4 * GP], "float32"),
+    "rl": ("sbuf", [128, GW], "float32"),
+    "bl": ("sbuf", [128, NR * W], "float32"),
+    "gt": ("sbuf", [128, RK * PW], "float32"),
+    "yb": ("sbuf", [128, NR * W], "float32"),
     "ht": ("sbuf", [16, 2], "int32"),
     "hb": ("sbuf", [128, 2], "int32"),
     "pi": ("sbuf", [128, 1], "int32"),
@@ -21,20 +29,21 @@ SCRATCH = {
     "hf": ("sbuf", [128, 1], "float32"),
     "sq": ("sbuf", [128, 2], "int32"),
     "sf": ("sbuf", [128, 2], "float32"),
-    "r6": ("sbuf", [128, RK * PAD // 16], "float32"),
-    "dd": ("sbuf", [128, RK * PAD // 16], "float32"),
-    "u1": ("sbuf", [128, RK * PAD // 16], "float32"),
-    "u2": ("sbuf", [128, RK * PAD // 16], "float32"),
-    "u3": ("sbuf", [128, RK * PAD // 16], "float32"),
-    "jj": ("sbuf", [128, 64], "float32"),
-    "ji": ("sbuf", [128, 64], "int32"),
-    "jr": ("sbuf", [128, 64], "int32"),
-    "offi": ("sbuf", [128, RK * PAD // 16], "uint16"),
-    "offl": ("sbuf", [128, 64], "uint16"),
-    "offf": ("sbuf", [128, 64], "uint16"),
+    "jj": ("sbuf", [128, 4 * GO], "float32"),
+    "ji": ("sbuf", [128, 4 * GO], "int32"),
+    "jr": ("sbuf", [128, 4 * GO], "int32"),
+    "offs": ("sbuf", [128, 4 * GO], "uint16"),
+    "pt": ("sbuf", [128, NT], "float32"),
+    "o16": ("sbuf", [128, 2], "uint16"),
+    "pl": ("sbuf", [128, 16], "float32"),
+    "dp": ("sbuf", [128, RK], "float32"),
+    "bs": ("sbuf", [128, RK * n], "float32"),
+    "cy": ("sbuf", [128, n], "float32"),
+    "uu": ("sbuf", [128, RK * n], "float32"),
+    "offi": ("sbuf", [128, RK * n], "uint16"),
 }
-SEMAPHORES = ["lh", "lxr", "lxa", "lxb", "lxo", "tab", "hb", "v", "li", "lf", "fl", "arrr", "arr1", "arr2", "arr3", "ls", "gv",
-              "ga", "own", "f0", "f1", "f2", "st"]
+SEMAPHORES = ["lh", "lx", "lxo", "tab", "hb", "v", "fl", "s1", "s2", "s3", "lp", "li", "arrr", "arrn", "arrf", "arr2", "ls",
+              "g1", "gv", "ga", "e0", "e1", "t0", "t1", "st"]
 
 
 def bits(mask):
@@ -45,9 +54,9 @@ def to_mask(bs):
     return sum(1 << b for b in bs)
 
 
-def deal(engines, n):
+def deal(engines, k):
     e = len(engines)
-    cut = {1: [e], 2: [e // 2, e // 2], 3: [e // 4, e // 4, e // 2], 4: [e // 4] * 4}[n]
+    cut = {1: [e], 2: [e // 2, e // 2], 3: [e // 4, e // 4, e // 2], 4: [e // 4] * 4}[k]
     out, at = [], 0
     for c in cut:
         out.append(to_mask(engines[at:at + c]))
@@ -69,33 +78,34 @@ def layout(T, topo):
         first = c - c % 8
         helper.append([d for d in range(first, first + 8) if topo.chip(d) == topo.chip(c) and topo.die(d) != topo.die(c)
                        and all(topo.may_write(d, cores[p]) for p in racks[side[r]])][0])
-    width0 = []
-    for r in racks[0]:
-        kin = [p for p in racks[0] if topo.same_plane(cores[p], cores[r])]
-        width0.append(W_SMALL if len(kin) < 2 else W_BIG)
-    lo0 = [RK * WH + sum(width0[:i]) for i in range(RK)]
     near_host = [[p for p in racks[side[r]] if topo.host(cores[p]) == topo.host(cores[r])] for r in ranks]
     far_host = [[p for p in racks[side[r]] if topo.host(cores[p]) != topo.host(cores[r])] for r in ranks]
     far = bits(topo.mask(cores[0], cores[1]))
-    near = [b for b in bits(topo.mask(cores[0], helper[0])) if b not in far][::2]
+    near = [b for b in bits(topo.mask(cores[0], helper[0])) if b not in far]
     return {"cores": cores, "racks": racks, "side": side, "partner": partner, "label": label, "helper": helper,
-            "width0": width0, "lo0": lo0, "far": far, "near": near, "near_host": near_host, "far_host": far_host}
+            "far": far, "near": near, "near_host": near_host, "far_host": far_host}
 
 
-def slice_of(L, lane, r):
-    k = L["label"][r]
-    return (k * WH, (k + 1) * WH) if lane else (L["lo0"][k], L["lo0"][k] + L["width0"][k])
+def slot_of(lane, k):
+    return (0 if lane else RK * W) + k * W
 
 
-def span_of(L, group):
-    ks = [L["label"][r] for r in group]
-    return min(ks) * WH, (max(ks) + 1) * WH
+def list_of(lane, group):
+    return (0 if lane else 2) + group
+
+
+def turned(lane, k):
+    return list_of(lane, k // HR) * GP + (k % HR) * W
 
 
 def place_of(L, q, r):
-    s = L["side"][q]
-    mine = r if L["side"][r] == s else L["partner"][r]
-    return RK * s + (q - mine - 1) % RK
+    base = 0
+    me = r
+    if L["side"][q] != L["side"][r]:
+        base, me = RK, L["partner"][r]
+    if q in L["near_host"][me]:
+        return base + (L["label"][q] - L["label"][me]) % HR
+    return base + HR + L["label"][q] % HR
 
 
 def peers_of(L, r):
@@ -106,29 +116,28 @@ def peers_of(L, r):
 
 def hop1_calls(L, r):
     peers = peers_of(L, r)
-    grp = [p for p in peers if p in L["near_host"][r]] + [L["partner"][r], r]
-    calls = [(1, list(zip(grp, deal(L["far"], len(grp)))))]
-    for w in (W_BIG, W_SMALL):
-        grp = [p for p in peers + [L["partner"][r]] if L["width0"][L["label"][p]] == w]
-        calls.append((0, list(zip(grp, deal(L["far"], len(grp))))))
+    near = [p for p in peers if p in L["near_host"][r]]
+    far = [p for p in peers if p in L["far_host"][r]]
+    pal = L["partner"][r]
+    a = [(1, p) for p in near] + [(0, p) for p in near]
+    b = [(0, p) for p in far] + [(0, pal)]
+    calls = [[(ln, p, mk) for (ln, p), mk in zip(grp, deal(L["far"], 4))] for grp in (a, b)]
+    calls.append([(1, pal, to_mask(L["far"])), (1, r, to_mask(L["near"]))])
     return calls
 
 
-def relay_calls(L, r):
+def relay_call(L, r):
     grp = [p for p in peers_of(L, r) if p in L["far_host"][r]]
-    return [(1, list(zip(grp, deal(L["far"], len(grp)))))]
+    return [(1, p, mk) for p, mk in zip(grp, deal(L["far"], len(grp)))]
 
 
 def hop3_calls(L, lane, r):
     peers = peers_of(L, r)
     first = list(zip(peers[:4], deal(L["far"], 4)))
+    last = [(peers[4], to_mask(L["far"]))]
     if lane:
-        first.append((r, to_mask(L["near"])))
-    return [first, [(peers[4], to_mask(L["far"]))]]
-
-
-def arrivals(calls, r):
-    return sum(len(bits(mk)) for call in calls for d, mk in call if d == r)
+        last.append((r, to_mask(L["near"][::2])))
+    return [first, last]
 
 
 def rank_program(g, core, T, topo):
@@ -141,18 +150,19 @@ def rank_program(g, core, T, topo):
     else:
         return
     S = T.sem
-    V, A = g.vector, g.scalar
+    V, A, Y = g.vector, g.scalar, g.sync
     copy = ActivationFunctionType.Copy
-    side = L["side"][rank]
-    rack = L["racks"][side]
+    add, mult = AluOpType.add, AluOpType.mult
+    rack = L["racks"][L["side"][rank]]
     pal = L["partner"][rank]
     home = cores[rank]
     helper = L["helper"][rank]
     where = [[cores[r] for r in range(NR)], L["helper"]]
-    lo, hi = slice_of(L, lane, rank)
-    W = hi - lo
-    n = (W + 15) // 16
-    PW = 16 * n
+    label = L["label"]
+    k = label[rank]
+    mine, other = k // HR, 1 - k // HR
+    lo = slot_of(lane, k)
+    far8, near8 = to_mask(L["far"]), to_mask(L["near"])
     sent = [0]
 
     def fused(items):
@@ -164,45 +174,35 @@ def rank_program(g, core, T, topo):
             sent[0] += len(bits(mk))
         g.remote_dma_fused(ts, local_sem=S.ls)
 
-    def slices(calls, before):
-        for i, (ln, call) in enumerate(calls):
-            if i in before:
-                g.wait_ge(*before[i])
-            items = []
-            for d, mk in call:
-                a, b = slice_of(L, ln, d)
-                p = place_of(L, rank, d)
-                items.append((where[ln][d], mk, S.arr2 if d == pal else S.arr1, T.xs[:, a:b],
-                              T.bl[:, p * (b - a):(p + 1) * (b - a)]))
-            fused(items)
+    def group_sem(src, dst):
+        if src != dst and src in L["near_host"][dst]:
+            return "arrn"
+        return "arrf" if src in L["far_host"][dst] else "arr2"
 
-    ra, rb = span_of(L, L["far_host"][rank])
+    def count(sem):
+        got = 0
+        for r in range(NR):
+            for call in hop1_calls(L, r) + [relay_call(L, r)]:
+                got += sum(len(bits(mk)) for ln, d, mk in call if (ln, d) == (lane, rank) and group_sem(r, d) == sem)
+        return got
+
+    def slices(call, source):
+        items = []
+        for ln, d, mk in call:
+            p = place_of(L, rank, d)
+            a = source(ln, label[d])
+            buf = T.gs if lane == 0 else T.rl
+            items.append((where[ln][d], mk, S[group_sem(rank, d)], buf[:, a:a + W], T.bl[:, p * W:(p + 1) * W]))
+        fused(items)
+
     if lane == 0:
-        na, nb = span_of(L, L["near_host"][rank])
-        h2, c1 = RK * WH, (RK * WH + TC) // 2
-        p = place_of(L, rank, rank)
-        g.sync.dma_start(out=T.ht[:], in_=T.hh[:]).then_inc(S.lh, 16)
-        A.dma_start(out=T.xs[:, ra:rb], in_=T.x[:, ra:rb]).then_inc(S.lxr, 16)
-        g.sync.dma_start(out=T.xs[:, na:nb], in_=T.x[:, na:nb]).then_inc(S.lxa, 16)
-        A.dma_start(out=T.xs[:, h2:c1], in_=T.x[:, h2:c1]).then_inc(S.lxb, 16)
-        g.sync.dma_start(out=T.xs[:, c1:TC], in_=T.x[:, c1:TC]).then_inc(S.lxb, 16)
-        A.dma_start(out=T.bl[:, p * W:(p + 1) * W], in_=T.x[:, lo:hi]).then_inc(S.lxo, 16)
+        A.dma_start(out=T.xs[:], in_=T.x[:]).then_inc(S.lx, 16)
+        Y.dma_start(out=T.ht[:], in_=T.hh[:]).then_inc(S.lh, 16)
 
     g.iota(T.pi[:], [[0, 1]], 0, 1).then_inc(S.tab, 1)
-    if lane == 1:
-        g.iota(T.jj[:], [[16, 64]], 0, 0, allow_small_or_imprecise_dtypes=True).then_inc(S.tab, 1)
-    g.iota(T.r6[:, 0:RK * n], [[0, RK], [16, n]], lo, 0, allow_small_or_imprecise_dtypes=True).then_inc(S.tab, 1)
-    g.iota(T.dd[:, 0:RK * n], [[1, RK], [0, n]], rack[0], 0, allow_small_or_imprecise_dtypes=True).then_inc(S.tab, 1)
-
     if lane == 0:
-        g.wait_ge(S.lh, 16)
-        g.partition_broadcast(T.hb[:], T.ht[0:1, :], 128).then_inc(S.hb, 1)
-        g.wait_ge(S.hb, 1)
-        fused([(helper, to_mask(L["far"]), S.hb, T.hb[:], T.hb[:])])
-        g.wait_ge(S.lxr, 16)
-        fused([(helper, to_mask(L["near"]), S.arrr, T.xs[:, ra:rb], T.xs[:, ra:rb])])
-        slices(hop1_calls(L, rank), {0: (S.lxa, 16), 1: (S.lxb, 32)})
-    hb_in = 1 if lane == 0 else len(L["far"])
+        g.iota(T.jj[:], [[GW, 4], [16, GO]], 0, 0, allow_small_or_imprecise_dtypes=True).then_inc(S.tab, 1)
+    g.iota(T.bs[:], [[0, RK], [16, n]], 0, 0, allow_small_or_imprecise_dtypes=True).then_inc(S.tab, 1)
 
     nv = [0]
 
@@ -213,104 +213,149 @@ def rank_program(g, core, T, topo):
     def sync_v():
         V.wait_ge(S.v, nv[0])
 
-    r6, dd, u1, u2, u3 = (t[:, 0:RK * n] for t in (T.r6, T.dd, T.u1, T.u2, T.u3))
-    V.wait_ge(S.tab, 3 + lane)
+    if lane == 1:
+        for e in range(NT):
+            step(V.memset(T.pt[:, e:e + 1], float(W * place_of(L, (rack[0] + e) % NR, rank))))
+    V.wait_ge(S.tab, 3 - lane)
     step(V.tensor_scalar(T.pi[:], T.pi[:], 15, None, AluOpType.bitwise_and))
     sync_v()
     step(V.tensor_copy(T.pf[:], T.pi[:]))
     sync_v()
-    step(V.tensor_scalar(r6, r6, T.pf[:], None, AluOpType.add))
-    V.wait_ge(S.hb, hb_in)
-    if lane == 1:
-        step(V.tensor_copy(T.hf[:], T.hb[:, 0:1]))
-        sync_v()
-        step(V.tensor_scalar(T.ji[:], T.jj[:], T.pf[:], T.hf[:], AluOpType.add, AluOpType.add))
-        sync_v()
-        step(V.tensor_scalar(T.jr[:], T.ji[:], TC - 1, None, AluOpType.bitwise_and))
-        sync_v()
-        V.tensor_copy(T.offl[:], T.jr[:]).then_inc(S.fl, 1)
-        g.wait_ge(S.fl, 1)
-        fused([(home, to_mask(L["far"]), S.lf, T.offl[:], T.offf[:])])
-        g.wait_ge(S.arrr, len(L["near"]))
-        slices(relay_calls(L, rank), {})
-    step(V.tensor_scalar(T.sq[:, 0:1], T.hb[:, 0:1], TC - 1, None, AluOpType.bitwise_and))
-    step(V.tensor_scalar(T.sq[:, 1:2], T.hb[:, 0:1], 10, None, AluOpType.logical_shift_right))
-    sync_v()
-    step(V.tensor_copy(T.sf[:], T.sq[:]))
-    sync_v()
-    step(V.tensor_scalar(u1, r6, T.sf[:, 0:1], T.sf[:, 1:2], AluOpType.is_lt, AluOpType.add))
-    sync_v()
-    step(V.tensor_tensor(u1, u1, dd, AluOpType.add))
-    sync_v()
-    step(V.tensor_scalar(u2, u1, float(NR), float(-NR), AluOpType.is_ge, AluOpType.mult))
-    sync_v()
-    step(V.tensor_tensor(u1, u1, u2, AluOpType.add))
-    sync_v()
-    mine = [rank if side == k else pal for k in (0, 1)]
-    a0, a1 = (mine[k] - L["racks"][k][0] + 1 for k in (0, 1))
-    step(V.tensor_scalar(u2, u1, float(RK), float(-(a1 - a0 + RK)), AluOpType.is_ge, AluOpType.mult))
-    step(V.tensor_scalar(u3, u1, float(RK), float(RK), AluOpType.is_ge, AluOpType.mult))
-    sync_v()
-    step(V.tensor_tensor(u1, u1, u2, AluOpType.add))
-    sync_v()
-    step(V.tensor_scalar(u2, u1, float(a0), float(RK), AluOpType.is_lt, AluOpType.mult))
-    step(V.tensor_tensor(u1, u1, u3, AluOpType.add))
-    sync_v()
-    step(V.tensor_tensor(u1, u1, u2, AluOpType.add))
-    sync_v()
-    step(V.tensor_scalar(u1, u1, float(W), None, AluOpType.mult))
-    sync_v()
-    step(V.tensor_tensor(u1, u1, r6, AluOpType.add))
-    sync_v()
-    V.tensor_scalar(T.offi[:, 0:RK * n], u1, float(-(lo + W * a0)), float(NR * W - 1), AluOpType.add,
-                    AluOpType.min).then_inc(S.li, 1)
+    step(V.tensor_scalar(T.bs[:], T.bs[:], T.pf[:], None, add))
 
     if lane == 0:
-        n1 = sum(arrivals([c for ln, c in hop1_calls(L, r) if ln == 0], rank) for r in rack)
-    else:
-        n1 = sum(arrivals([c for ln, c in hop1_calls(L, r) if ln == 1] + [c for ln, c in relay_calls(L, r)], rank)
-                 for r in rack)
-    n2 = len(L["far"]) + arrivals([c for ln, c in hop1_calls(L, pal) if ln == lane], rank)
-    g.wait_ge(S.arr1, n1)
-    five = T.bl[:, RK * side * W:(RK * side + RK - 1) * W]
-    fused([(where[lane][pal], to_mask(L["far"]), S.arr2, five, five)])
+        g.wait_ge(S.lh, 16)
+        g.partition_broadcast(T.hb[:], T.ht[0:1, :], 128).then_inc(S.hb, 1)
+        g.wait_ge(S.hb, 1)
+        fused([(helper, near8, S.hb, T.hb[:], T.hb[:])])
+    V.wait_ge(S.hb, 1 if lane == 0 else len(L["near"]))
 
-    cut = 3 if (3 * n) % 2 == 0 else 4
-    win = T.bl[:, 0:NR * W]
+    if lane == 0:
+        step(V.tensor_copy(T.hf[:], T.hb[:, 0:1]))
+        sync_v()
+        step(V.tensor_scalar(T.ji[:], T.jj[:], T.pf[:], T.hf[:], add, add))
+        sync_v()
+        step(V.tensor_scalar(T.jr[:], T.ji[:], TC - 1, None, AluOpType.bitwise_and))
+        step(V.tensor_scalar(T.sq[:, 0:1], T.hb[:, 0:1], TC - 1, None, AluOpType.bitwise_and))
+        sync_v()
+        V.tensor_copy(T.offs[:], T.jr[:]).then_inc(S.fl, 1)
+        for q in (V, A):
+            q.wait_ge(S.fl, 1)
+            q.wait_ge(S.lx, 16)
+
+        def turn(q, i, a, b):
+            out, src = T.gs[:, i * GP + 16 * a:i * GP + 16 * b], T.xs[:].indirect(T.offs[:, i * GO + a:i * GO + b])
+            return V.tensor_copy(out, src) if q is V else A.activation(out, src, copy)
+
+        turn(V, list_of(1, other), 0, CUT).then_inc(S.s1, 1)
+        turn(A, list_of(1, other), CUT, GC).then_inc(S.s1, 1)
+        turn(V, list_of(0, mine), 0, GC).then_inc(S.s2, 1)
+        turn(A, list_of(1, mine), 0, GC).then_inc(S.s2, 1)
+        turn(V, list_of(0, other), 0, CUT).then_inc(S.s3, 1)
+        turn(A, list_of(0, other), CUT, GC).then_inc(S.s3, 1)
+
+        g.wait_ge(S.s1, 2)
+        a = list_of(1, other) * GP
+        fused([(helper, near8, S.arrr, T.gs[:, a:a + GW], T.rl[:])])
+        for call, sem in zip(hop1_calls(L, rank), (S.s2, S.s3, None)):
+            if sem is not None:
+                g.wait_ge(sem, 2)
+            slices(call, turned)
+        a = turned(0, k)
+        Y.wait_ge(S.s2, 2)
+        Y.dma_start(out=T.bl[:, 0:W], in_=T.gs[:, a:a + W]).then_inc(S.lxo, 16)
+    else:
+        step(V.tensor_scalar(T.sq[:, 0:1], T.hb[:, 0:1], TC - 1, None, AluOpType.bitwise_and))
+        step(V.tensor_scalar(T.sq[:, 1:2], T.hb[:, 0:1], 10, None, AluOpType.logical_shift_right))
+        sync_v()
+        step(V.tensor_copy(T.sf[:], T.sq[:]))
+        sync_v()
+        step(V.tensor_scalar(T.o16[:, 0:1], T.pf[:], T.sf[:, 1:2], None, add))
+        sync_v()
+        V.tensor_copy(T.pl[:], T.pt[:].indirect(T.o16[:, 0:1])).then_inc(S.lp, 1)
+        g.wait_ge(S.lp, 1)
+        fused([(home, far8, S.lp, T.pl[:], T.pl[:])])
+        g.wait_ge(S.arrr, len(L["near"]))
+        slices(relay_call(L, rank), lambda ln, kd: (kd % HR) * W)
+
+    order = peers_of(L, rank) + [rank]
+    if lane == 0:
+        step(V.tensor_copy(T.sf[:, 0:1], T.sq[:, 0:1]))
+        sync_v()
+    step(V.tensor_scalar(T.cy[:], T.bs[:, 0:n], T.sf[:, 0:1], float(TC - lo), add, AluOpType.is_ge))
+    V.wait_ge(S.lp, 1 if lane == 1 else len(L["far"]))
+    step(V.tensor_tensor(T.dp[:], T.pl[:, 1:RK + 1], T.pl[:, 0:RK], AluOpType.subtract))
+    sync_v()
+    for i, d in enumerate(order):
+        j = rack.index(d)
+        step(V.tensor_scalar(T.uu[:, i * n:(i + 1) * n], T.cy[:], T.dp[:, j:j + 1], T.pl[:, j:j + 1], mult, add))
+    sync_v()
+    step(V.tensor_tensor(T.uu[:], T.uu[:], T.bs[:], add))
+    sync_v()
+    V.tensor_scalar(T.offi[:], T.uu[:], float(NR * W - 1), None, AluOpType.min).then_inc(S.li, 1)
+
+    for sem, a, b in (("arrn", 1, HR), ("arrf", HR, RK)):
+        g.wait_ge(S[sem], count(sem))
+        fused([(where[lane][pal], far8, S.arr2, T.bl[:, a * W:b * W], T.bl[:, (RK + a) * W:(RK + b) * W])])
+    n2 = count("arr2") + 2 * len(L["far"])
+
     for q in (V, A):
         q.wait_ge(S.li, 1)
-        q.wait_ge(S.arr1, n1)
+        q.wait_ge(S.arrn, count("arrn"))
+        q.wait_ge(S.arrf, count("arrf"))
         if lane == 0:
             q.wait_ge(S.lxo, 16)
         q.wait_ge(S.arr2, n2)
-    V.tensor_copy(T.gt[:, 0:cut * PW], win.indirect(T.offi[:, 0:cut * n])).then_inc(S.gv, 1)
-    A.activation(T.gt[:, cut * PW:RK * PW], win.indirect(T.offi[:, cut * n:RK * n]), copy).then_inc(S.ga, 1)
 
-    g.wait_ge(S.gv, 1)
-    g.wait_ge(S.ga, 1)
-    for call in hop3_calls(L, lane, rank):
-        fused([(cores[d], mk, S.arr3, T.gt[:, rack.index(d) * PW:rack.index(d) * PW + W], T.rv[:, lo:hi]) for d, mk in call])
+    def pick(q, a, b):
+        out, src = T.gt[:, a * PW:b * PW], T.bl[:].indirect(T.offi[:, a * n:b * n])
+        return V.tensor_copy(out, src) if q is V else A.activation(out, src, copy)
+
+    pick(V, 0, 2).then_inc(S.g1, 1)
+    pick(A, 2, 4).then_inc(S.g1, 1)
+    pick(V, 4, 5).then_inc(S.gv, 1)
+    pick(A, 5, 6).then_inc(S.ga, 1)
+
+    for c, call in enumerate(hop3_calls(L, lane, rank)):
+        if c == 0:
+            g.wait_ge(S.g1, 2)
+        else:
+            g.wait_ge(S.gv, 1)
+            if lane == 1:
+                g.wait_ge(S.ga, 1)
+        sem = S["%s%d" % ("et"[c], lane)]
+        fused([(cores[d], mk, sem, T.gt[:, order.index(d) * PW:order.index(d) * PW + W], T.yb[:, lo:lo + W])
+               for d, mk in call])
 
     if lane == 0:
-        k = rack.index(rank)
-        V.wait_ge(S.gv, 1)
-        V.wait_ge(S.ga, 1)
-        V.tensor_copy(T.rv[:, lo:hi], T.gt[:, k * PW:k * PW + W]).then_inc(S.own, 1)
-        n3 = sum(arrivals(hop3_calls(L, ln, r), rank) for r in rack for ln in (0, 1))
-        for q in (V, A):
-            q.wait_ge(S.lf, len(L["far"]))
-            q.wait_ge(S.own, 1)
-            q.wait_ge(S.arr3, n3)
-        V.tensor_copy(T.yb[:, 0:256], T.rv[:].indirect(T.offf[:, 0:16])).then_inc(S.f0, 1)
-        V.tensor_copy(T.yb[:, 256:512], T.rv[:].indirect(T.offf[:, 16:32])).then_inc(S.f1, 1)
-        A.activation(T.yb[:, 512:1024], T.rv[:].indirect(T.offf[:, 32:64]), copy).then_inc(S.f2, 1)
-        g.sync.wait_ge(S.f0, 1)
-        g.sync.dma_start(out=T.y[:, 0:256], in_=T.yb[:, 0:256]).then_inc(S.st, 16)
-        g.sync.wait_ge(S.f1, 1)
-        g.sync.dma_start(out=T.y[:, 256:512], in_=T.yb[:, 256:512]).then_inc(S.st, 16)
-        A.wait_ge(S.f2, 1)
-        A.dma_start(out=T.y[:, 512:1024], in_=T.yb[:, 512:1024]).then_inc(S.st, 16)
+        stores = [0]
+
+        def store(q, out, src):
+            q.dma_start(out=out, in_=src).then_inc(S.st, 16)
+            stores[0] += 16
+
+        A.wait_ge(S.ga, 1)
+        hi = min(lo + W, TC)
+        store(A, T.y[:, lo:hi], T.gt[:, (RK - 1) * PW:(RK - 1) * PW + hi - lo])
+        for ln, q in ((1, Y), (0, A)):
+            for c in (0, 1):
+                got, labels = 0, []
+                for r in rack:
+                    for d, mk in hop3_calls(L, ln, r)[c]:
+                        if d == rank:
+                            got += len(bits(mk))
+                            labels.append(label[r])
+                labels.sort()
+                q.wait_ge(S["%s%d" % ("et"[c], ln)], got)
+                i = 0
+                while i < len(labels):
+                    e = i
+                    while e + 1 < len(labels) and labels[e + 1] == labels[e] + 1:
+                        e += 1
+                    a, b = slot_of(ln, labels[i]), min(slot_of(ln, labels[e]) + W, TC)
+                    store(q, T.y[:, a:b], T.yb[:, a:b])
+                    i = e + 1
     V.wait_ge(S.v, nv[0])
     g.wait_ge(S.ls, sent[0])
     if lane == 0:
-        g.wait_ge(S.st, 48)
+        g.wait_ge(S.st, stores[0])

from concourse.bass import DstId, RemoteDMATransfer
from concourse.mybir import AluOpType, ActivationFunctionType

NR = 12
TC = 1024
RK = 6
HR = 3
W = 86
n = 6
PW = 16 * n
GW = HR * W
GC = 17
GP = 16 * GC
GO = 18
CUT = 10
NT = NR + 15

SCRATCH = {
    "xs": ("sbuf", [128, TC], "float32"),
    "gs": ("sbuf", [128, 4 * GP], "float32"),
    "rl": ("sbuf", [128, GW], "float32"),
    "bl": ("sbuf", [128, NR * W], "float32"),
    "gt": ("sbuf", [128, RK * PW], "float32"),
    "yb": ("sbuf", [128, NR * W], "float32"),
    "ht": ("sbuf", [16, 2], "int32"),
    "hb": ("sbuf", [128, 2], "int32"),
    "pi": ("sbuf", [128, 1], "int32"),
    "pf": ("sbuf", [128, 1], "float32"),
    "hf": ("sbuf", [128, 1], "float32"),
    "sq": ("sbuf", [128, 2], "int32"),
    "sf": ("sbuf", [128, 2], "float32"),
    "jj": ("sbuf", [128, 4 * GO], "float32"),
    "ji": ("sbuf", [128, 4 * GO], "int32"),
    "jr": ("sbuf", [128, 4 * GO], "int32"),
    "offs": ("sbuf", [128, 4 * GO], "uint16"),
    "pt": ("sbuf", [128, NT], "float32"),
    "o16": ("sbuf", [128, 2], "uint16"),
    "pl": ("sbuf", [128, 16], "float32"),
    "dp": ("sbuf", [128, RK], "float32"),
    "bs": ("sbuf", [128, RK * n], "float32"),
    "cy": ("sbuf", [128, n], "float32"),
    "uu": ("sbuf", [128, RK * n], "float32"),
    "offi": ("sbuf", [128, RK * n], "uint16"),
}
SEMAPHORES = ["lh", "lx", "lxo", "tab", "hb", "v", "fl", "s1", "s2", "s3", "lp", "li", "arrr", "arrn", "arrf", "arr2", "ls",
              "g1", "gv", "ga", "e0", "e1", "t0", "t1", "st"]


def bits(mask):
    return [b for b in range(16) if mask >> b & 1]


def to_mask(bs):
    return sum(1 << b for b in bs)


def deal(engines, k):
    e = len(engines)
    cut = {1: [e], 2: [e // 2, e // 2], 3: [e // 4, e // 4, e // 2], 4: [e // 4] * 4}[k]
    out, at = [], 0
    for c in cut:
        out.append(to_mask(engines[at:at + c]))
        at += c
    return out


def layout(T, topo):
    cores = T.cores
    ranks = list(range(NR))
    racks = [[r for r in ranks if topo.rack(topo.host(cores[r])) == k] for k in (0, 1)]
    side = [0 if r in racks[0] else 1 for r in ranks]
    partner = [[p for p in ranks if side[p] != side[r] and topo.chip(cores[p]) == topo.chip(cores[r])
                and topo.may_write(cores[r], cores[p])][0] for r in ranks]
    label = [racks[0].index(r if side[r] == 0 else partner[r]) for r in ranks]
    helper = []
    for r in ranks:
        c = cores[r]
        first = c - c % 8
        helper.append([d for d in range(first, first + 8) if topo.chip(d) == topo.chip(c) and topo.die(d) != topo.die(c)
                       and all(topo.may_write(d, cores[p]) for p in racks[side[r]])][0])
    near_host = [[p for p in racks[side[r]] if topo.host(cores[p]) == topo.host(cores[r])] for r in ranks]
    far_host = [[p for p in racks[side[r]] if topo.host(cores[p]) != topo.host(cores[r])] for r in ranks]
    far = bits(topo.mask(cores[0], cores[1]))
    near = [b for b in bits(topo.mask(cores[0], helper[0])) if b not in far]
    return {"cores": cores, "racks": racks, "side": side, "partner": partner, "label": label, "helper": helper,
            "far": far, "near": near, "near_host": near_host, "far_host": far_host}


def slot_of(lane, k):
    return (0 if lane else RK * W) + k * W


def list_of(lane, group):
    return (0 if lane else 2) + group


def turned(lane, k):
    return list_of(lane, k // HR) * GP + (k % HR) * W


def place_of(L, q, r):
    base = 0
    me = r
    if L["side"][q] != L["side"][r]:
        base, me = RK, L["partner"][r]
    if q in L["near_host"][me]:
        return base + (L["label"][q] - L["label"][me]) % HR
    return base + HR + L["label"][q] % HR


def peers_of(L, r):
    rack = L["racks"][L["side"][r]]
    k = rack.index(r)
    return [rack[(k + i) % RK] for i in range(1, RK)]


def hop1_calls(L, r):
    peers = peers_of(L, r)
    near = [p for p in peers if p in L["near_host"][r]]
    far = [p for p in peers if p in L["far_host"][r]]
    pal = L["partner"][r]
    a = [(1, p) for p in near] + [(0, p) for p in near]
    b = [(0, p) for p in far] + [(0, pal)]
    calls = [[(ln, p, mk) for (ln, p), mk in zip(grp, deal(L["far"], 4))] for grp in (a, b)]
    calls.append([(1, pal, to_mask(L["far"])), (1, r, to_mask(L["near"]))])
    return calls


def relay_call(L, r):
    grp = [p for p in peers_of(L, r) if p in L["far_host"][r]]
    return [(1, p, mk) for p, mk in zip(grp, deal(L["far"], len(grp)))]


def hop3_calls(L, lane, r):
    peers = peers_of(L, r)
    first = list(zip(peers[:4], deal(L["far"], 4)))
    last = [(peers[4], to_mask(L["far"]))]
    if lane:
        last.append((r, to_mask(L["near"][::2])))
    return [first, last]


def rank_program(g, core, T, topo):
    L = layout(T, topo)
    cores = L["cores"]
    if core in cores:
        lane, rank = 0, cores.index(core)
    elif core in L["helper"]:
        lane, rank = 1, L["helper"].index(core)
    else:
        return
    S = T.sem
    V, A, Y = g.vector, g.scalar, g.sync
    copy = ActivationFunctionType.Copy
    add, mult = AluOpType.add, AluOpType.mult
    rack = L["racks"][L["side"][rank]]
    pal = L["partner"][rank]
    home = cores[rank]
    helper = L["helper"][rank]
    where = [[cores[r] for r in range(NR)], L["helper"]]
    label = L["label"]
    k = label[rank]
    mine, other = k // HR, 1 - k // HR
    lo = slot_of(lane, k)
    far8, near8 = to_mask(L["far"]), to_mask(L["near"])
    sent = [0]

    def fused(items):
        ts = []
        for dst, mk, sem, src, out in items:
            rid, pid = topo.addr(dst, core)
            ts.append(RemoteDMATransfer(dst_ids=[DstId(rid=rid, pnc=pid)], dma_engine_mask=mk, remote_sem=sem,
                                        srcs=[src], dsts=[out]))
            sent[0] += len(bits(mk))
        g.remote_dma_fused(ts, local_sem=S.ls)

    def group_sem(src, dst):
        if src != dst and src in L["near_host"][dst]:
            return "arrn"
        return "arrf" if src in L["far_host"][dst] else "arr2"

    def count(sem):
        got = 0
        for r in range(NR):
            for call in hop1_calls(L, r) + [relay_call(L, r)]:
                got += sum(len(bits(mk)) for ln, d, mk in call if (ln, d) == (lane, rank) and group_sem(r, d) == sem)
        return got

    def slices(call, source):
        items = []
        for ln, d, mk in call:
            p = place_of(L, rank, d)
            a = source(ln, label[d])
            buf = T.gs if lane == 0 else T.rl
            items.append((where[ln][d], mk, S[group_sem(rank, d)], buf[:, a:a + W], T.bl[:, p * W:(p + 1) * W]))
        fused(items)

    if lane == 0:
        A.dma_start(out=T.xs[:], in_=T.x[:]).then_inc(S.lx, 16)
        Y.dma_start(out=T.ht[:], in_=T.hh[:]).then_inc(S.lh, 16)

    g.iota(T.pi[:], [[0, 1]], 0, 1).then_inc(S.tab, 1)
    if lane == 0:
        g.iota(T.jj[:], [[GW, 4], [16, GO]], 0, 0, allow_small_or_imprecise_dtypes=True).then_inc(S.tab, 1)
    g.iota(T.bs[:], [[0, RK], [16, n]], 0, 0, allow_small_or_imprecise_dtypes=True).then_inc(S.tab, 1)

    nv = [0]

    def step(ins):
        nv[0] += 1
        ins.then_inc(S.v, 1)

    def sync_v():
        V.wait_ge(S.v, nv[0])

    if lane == 1:
        for e in range(NT):
            step(V.memset(T.pt[:, e:e + 1], float(W * place_of(L, (rack[0] + e) % NR, rank))))
    V.wait_ge(S.tab, 3 - lane)
    step(V.tensor_scalar(T.pi[:], T.pi[:], 15, None, AluOpType.bitwise_and))
    sync_v()
    step(V.tensor_copy(T.pf[:], T.pi[:]))
    sync_v()
    step(V.tensor_scalar(T.bs[:], T.bs[:], T.pf[:], None, add))

    if lane == 0:
        g.wait_ge(S.lh, 16)
        g.partition_broadcast(T.hb[:], T.ht[0:1, :], 128).then_inc(S.hb, 1)
        g.wait_ge(S.hb, 1)
        fused([(helper, near8, S.hb, T.hb[:], T.hb[:])])
    V.wait_ge(S.hb, 1 if lane == 0 else len(L["near"]))

    if lane == 0:
        step(V.tensor_copy(T.hf[:], T.hb[:, 0:1]))
        sync_v()
        step(V.tensor_scalar(T.ji[:], T.jj[:], T.pf[:], T.hf[:], add, add))
        sync_v()
        step(V.tensor_scalar(T.jr[:], T.ji[:], TC - 1, None, AluOpType.bitwise_and))
        step(V.tensor_scalar(T.sq[:, 0:1], T.hb[:, 0:1], TC - 1, None, AluOpType.bitwise_and))
        sync_v()
        V.tensor_copy(T.offs[:], T.jr[:]).then_inc(S.fl, 1)
        for q in (V, A):
            q.wait_ge(S.fl, 1)
            q.wait_ge(S.lx, 16)

        def turn(q, i, a, b):
            out, src = T.gs[:, i * GP + 16 * a:i * GP + 16 * b], T.xs[:].indirect(T.offs[:, i * GO + a:i * GO + b])
            return V.tensor_copy(out, src) if q is V else A.activation(out, src, copy)

        turn(V, list_of(1, other), 0, CUT).then_inc(S.s1, 1)
        turn(A, list_of(1, other), CUT, GC).then_inc(S.s1, 1)
        turn(V, list_of(0, mine), 0, GC).then_inc(S.s2, 1)
        turn(A, list_of(1, mine), 0, GC).then_inc(S.s2, 1)
        turn(V, list_of(0, other), 0, CUT).then_inc(S.s3, 1)
        turn(A, list_of(0, other), CUT, GC).then_inc(S.s3, 1)

        g.wait_ge(S.s1, 2)
        a = list_of(1, other) * GP
        fused([(helper, near8, S.arrr, T.gs[:, a:a + GW], T.rl[:])])
        for call, sem in zip(hop1_calls(L, rank), (S.s2, S.s3, None)):
            if sem is not None:
                g.wait_ge(sem, 2)
            slices(call, turned)
        a = turned(0, k)
        Y.wait_ge(S.s2, 2)
        Y.dma_start(out=T.bl[:, 0:W], in_=T.gs[:, a:a + W]).then_inc(S.lxo, 16)
    else:
        step(V.tensor_scalar(T.sq[:, 0:1], T.hb[:, 0:1], TC - 1, None, AluOpType.bitwise_and))
        step(V.tensor_scalar(T.sq[:, 1:2], T.hb[:, 0:1], 10, None, AluOpType.logical_shift_right))
        sync_v()
        step(V.tensor_copy(T.sf[:], T.sq[:]))
        sync_v()
        step(V.tensor_scalar(T.o16[:, 0:1], T.pf[:], T.sf[:, 1:2], None, add))
        sync_v()
        V.tensor_copy(T.pl[:], T.pt[:].indirect(T.o16[:, 0:1])).then_inc(S.lp, 1)
        g.wait_ge(S.lp, 1)
        fused([(home, far8, S.lp, T.pl[:], T.pl[:])])
        g.wait_ge(S.arrr, len(L["near"]))
        slices(relay_call(L, rank), lambda ln, kd: (kd % HR) * W)

    order = peers_of(L, rank) + [rank]
    if lane == 0:
        step(V.tensor_copy(T.sf[:, 0:1], T.sq[:, 0:1]))
        sync_v()
    step(V.tensor_scalar(T.cy[:], T.bs[:, 0:n], T.sf[:, 0:1], float(TC - lo), add, AluOpType.is_ge))
    V.wait_ge(S.lp, 1 if lane == 1 else len(L["far"]))
    step(V.tensor_tensor(T.dp[:], T.pl[:, 1:RK + 1], T.pl[:, 0:RK], AluOpType.subtract))
    sync_v()
    for i, d in enumerate(order):
        j = rack.index(d)
        step(V.tensor_scalar(T.uu[:, i * n:(i + 1) * n], T.cy[:], T.dp[:, j:j + 1], T.pl[:, j:j + 1], mult, add))
    sync_v()
    step(V.tensor_tensor(T.uu[:], T.uu[:], T.bs[:], add))
    sync_v()
    V.tensor_scalar(T.offi[:], T.uu[:], float(NR * W - 1), None, AluOpType.min).then_inc(S.li, 1)

    for sem, a, b in (("arrn", 1, HR), ("arrf", HR, RK)):
        g.wait_ge(S[sem], count(sem))
        fused([(where[lane][pal], far8, S.arr2, T.bl[:, a * W:b * W], T.bl[:, (RK + a) * W:(RK + b) * W])])
    n2 = count("arr2") + 2 * len(L["far"])

    for q in (V, A):
        q.wait_ge(S.li, 1)
        q.wait_ge(S.arrn, count("arrn"))
        q.wait_ge(S.arrf, count("arrf"))
        if lane == 0:
            q.wait_ge(S.lxo, 16)
        q.wait_ge(S.arr2, n2)

    def pick(q, a, b):
        out, src = T.gt[:, a * PW:b * PW], T.bl[:].indirect(T.offi[:, a * n:b * n])
        return V.tensor_copy(out, src) if q is V else A.activation(out, src, copy)

    pick(V, 0, 2).then_inc(S.g1, 1)
    pick(A, 2, 4).then_inc(S.g1, 1)
    pick(V, 4, 5).then_inc(S.gv, 1)
    pick(A, 5, 6).then_inc(S.ga, 1)

    for c, call in enumerate(hop3_calls(L, lane, rank)):
        if c == 0:
            g.wait_ge(S.g1, 2)
        else:
            g.wait_ge(S.gv, 1)
            if lane == 1:
                g.wait_ge(S.ga, 1)
        sem = S["%s%d" % ("et"[c], lane)]
        fused([(cores[d], mk, sem, T.gt[:, order.index(d) * PW:order.index(d) * PW + W], T.yb[:, lo:lo + W])
               for d, mk in call])

    if lane == 0:
        stores = [0]

        def store(q, out, src):
            q.dma_start(out=out, in_=src).then_inc(S.st, 16)
            stores[0] += 16

        A.wait_ge(S.ga, 1)
        hi = min(lo + W, TC)
        store(A, T.y[:, lo:hi], T.gt[:, (RK - 1) * PW:(RK - 1) * PW + hi - lo])
        for ln, q in ((1, Y), (0, A)):
            for c in (0, 1):
                got, labels = 0, []
                for r in rack:
                    for d, mk in hop3_calls(L, ln, r)[c]:
                        if d == rank:
                            got += len(bits(mk))
                            labels.append(label[r])
                labels.sort()
                q.wait_ge(S["%s%d" % ("et"[c], ln)], got)
                i = 0
                while i < len(labels):
                    e = i
                    while e + 1 < len(labels) and labels[e + 1] == labels[e] + 1:
                        e += 1
                    a, b = slot_of(ln, labels[i]), min(slot_of(ln, labels[e]) + W, TC)
                    store(q, T.y[:, a:b], T.yb[:, a:b])
                    i = e + 1
    V.wait_ge(S.v, nv[0])
    g.wait_ge(S.ls, sent[0])
    if lane == 0:
        g.wait_ge(S.st, stores[0])
